import numpy as np
import ml_dtypes


def mxq(x, axis, fmt="e4m3"):
    dtype, down = {"e4m3": (ml_dtypes.float8_e4m3fn, 7), "e5m2": (ml_dtypes.float8_e5m2, 14)}[fmt]
    v = np.moveaxis(np.asarray(x, np.float32).astype(ml_dtypes.bfloat16).astype(np.float64), axis, -1)
    blocks = v.reshape(v.shape[:-1] + (-1, 32))
    amax = np.abs(blocks).max(-1, keepdims=True)
    byte = np.maximum(np.where(amax > 0, np.frexp(amax)[1] - 1 + 127, 0) - down, 1)
    scale = np.exp2(byte - 127.0)
    codes = (blocks / scale).astype(np.float32).astype(dtype).astype(np.float64)
    return np.moveaxis((codes * scale).reshape(v.shape), -1, axis)


WIDE = False


def mx_kscale(k):
    if not WIDE:
        return np.ones(k)
    levels = np.array([10, -10, 5, -5, 0])
    if k % 512:
        return np.exp2(np.random.permutation(np.resize(levels, k // 32))).repeat(32)
    a = np.empty((k // 512, 16))
    for p in range(k // 512):
        a[p, :8] = np.random.permutation(np.resize(levels, 8))
        for g in range(8):
            far = levels[np.abs(levels - a[p, g]) >= 10]
            a[p, g + 8] = far[np.random.randint(len(far))]
    return np.exp2(a.ravel()).repeat(32)


def f64(x):
    return np.asarray(x).astype(np.float64)


def striped(idx):
    return np.tile(idx.reshape(-1, 16).T, (8, 1)).astype(np.uint16)


def unstriped(offs):
    return offs[:16].T.reshape(-1).astype(np.int64)


def pack_weight(w):
    k, n = w.shape
    w = f64(np.asarray(w, np.float32).astype(ml_dtypes.bfloat16)).reshape(k // 32, 32, n)
    amax = np.abs(w).max(1)
    byte = np.clip(np.where(amax > 0, np.frexp(amax)[1] - 1 + 127 - 7, 1), 1, 254)
    scaled = (w * np.exp2(127.0 - byte)[:, None, :]).reshape(k, n).astype(np.float32)
    words = np.ascontiguousarray(scaled.reshape(k // 512, 128, 4, n).transpose(0, 1, 3, 2)).astype(ml_dtypes.float8_e4m3fn).view(np.uint8)
    return words, np.ascontiguousarray(byte.astype(np.uint8).reshape(k // 512, 16, n))


def unpack_weight(words, scales):
    g, p, n, _ = words.shape
    vals = np.ascontiguousarray(words).view(ml_dtypes.float8_e4m3fn).astype(np.float64) * np.repeat(np.exp2(scales.astype(np.float64) - 127.0), 8, axis=1)[..., None]
    return vals.transpose(0, 1, 3, 2).reshape(g * 512, n)


K, T, S, N = 512, 1024, 512, 256
P = 2 ** 7


def setup_inputs():
    n = np.random.standard_normal
    s = mx_kscale(K)[:, None]
    packed_w1 = pack_weight(n((K, N)) / np.sqrt(K) / s)
    return {
        "xT": (n((K, T)) * s).astype(np.float32),
        "gate": np.tile(np.random.uniform(0.2, 1.0, T), (P, 1)).astype(np.float32),
        "w1_words": packed_w1[0],
        "w1_scales": packed_w1[1],
        "offs": striped(np.random.permutation(T)[:S]),
    }


def reference(xT, gate, w1_words, w1_scales, offs):
    xq = mxq(f64(xT)[:, unstriped(offs)], 0, "e4m3")
    y = unpack_weight(w1_words, w1_scales).T @ xq
    g = f64(gate)[:1][:, unstriped(offs)]
    out = np.zeros((N, T))
    out[:, unstriped(offs)] = y * g
    return out

@@ -1,0 +1,123 @@
+from contextlib import ExitStack
+
+import concourse.mybir as mybir
+from concourse.masks import make_identity
+
+K, T, S, N = 512, 1024, 512, 256
+FLOPS = 2 * K * S * N
+BYTES = 4 * K * T + 4 * T + K * N + K * N // 32 + 2 * 128 * S // 16 + 4 * N * T
+
+F32 = mybir.dt.float32
+BF16 = mybir.dt.bfloat16
+I32 = mybir.dt.int32
+U32 = mybir.dt.uint32
+U16 = mybir.dt.uint16
+U8 = mybir.dt.uint8
+FP8X4 = mybir.dt.float8_e4m3fn_x4
+MULT = mybir.AluOpType.mult
+
+P = 128
+PACK = 4
+HALF_T = T // 2
+HALF_S = S // 2
+LIST_COLS = HALF_S // 16
+GATE_ROW = T // P
+VECTOR_SHARE = 352
+
+
+def tile_picked_modgate_linnone_l_kernel(tc, xT, gate, w1_words, w1_scales, offs, out):
+    nc = tc.nc
+    with ExitStack() as ctx:
+        sb = ctx.enter_context(tc.tile_pool(name="sb", bufs=1))
+        psum = ctx.enter_context(tc.psum_pool(name="psum", bufs=1))
+
+        gate_cols = sb.tile([P, GATE_ROW], F32, name="gate_cols")
+        nc.sync.dma_start(gate_cols[:], gate[0, :].rearrange("(n m) -> n m", m=GATE_ROW))
+        offsets = sb.tile([P, S // 16], U16, name="offsets")
+        nc.sync.dma_start(offsets[:], offs)
+
+        x_rows = xT.rearrange("(p j) t -> p j t", j=PACK)
+        raw = {}
+        for u in range(2):
+            for c in range(2):
+                raw[u, c] = sb.tile([P, 2, HALF_T], F32, name=f"raw{u}{c}")
+                nc.sync.dma_start(raw[u, c][:], x_rows[:, 2 * u : 2 * u + 2, c * HALF_T : (c + 1) * HALF_T])
+
+        w_codes = sb.tile([P, N], U32, name="w_codes", align_bytes=64)
+        nc.sync.dma_start(w_codes[:].bitcast(I32), w1_words[0].rearrange("p n t -> p (n t)").bitcast(I32))
+        w_scales = sb.tile([P, N], U8, name="w_scales", align_bytes=64)
+        nc.vector.memset(w_scales[:].bitcast(I32), 0)
+        for q in range(4):
+            nc.sync.dma_start(w_scales[32 * q : 32 * q + 4, :].bitcast(I32), w1_scales[0, 4 * q : 4 * q + 4, :].bitcast(I32))
+
+        placed = [sb.tile([P, T], F32, name=f"placed{b}") for b in range(N // P)]
+        for window in placed:
+            nc.vector.memset(window[:], 0.0)
+
+        identity = sb.tile([P, P], F32, name="identity")
+        make_identity(nc, identity[:])
+
+        gate_all = sb.tile([P, T], F32, name="gate_all")
+        gate_by_m = gate_all[:].rearrange("p (n m) -> p n m", m=GATE_ROW)
+        for half, engine_copy in enumerate((nc.vector.tensor_copy, nc.scalar.copy)):
+            spread = psum.tile([P, 4, P], F32, name=f"spread{half}")
+            for i in range(4):
+                m = 4 * half + i
+                nc.tensor.transpose(spread[:, i, :], gate_cols[:, m : m + 1].to_broadcast([P, P]), identity[:])
+            engine_copy(gate_by_m[:, :, 4 * half : 4 * half + 4], spread[:].rearrange("p m n -> p n m"))
+        scores = sb.tile([P, S], F32, name="scores")
+        nc.vector.tensor_copy(scores[:], gate_all[:].indirect(offsets[:]))
+
+        pairs = [sb.tile([P, T], U32, name=f"pairs{u}") for u in range(2)]
+
+        def round_pairs(engine_copy, u, c, lo, hi):
+            dst = pairs[u][:].bitcast(BF16).rearrange("p (t e) -> p t e", e=2)
+            engine_copy(dst[:, c * HALF_T + lo : c * HALF_T + hi, :], raw[u, c][:, :, lo:hi].rearrange("p e t -> p t e"))
+
+        picked = [sb.tile([P, HALF_S * 2], U32, name=f"picked{h}", align_bytes=64) for h in range(2)]
+
+        def gather_pairs(u, h):
+            nc.vector.tensor_copy(
+                picked[h][:].rearrange("p (s u) -> p s u", u=2)[:, :, u],
+                pairs[u][:].indirect(offsets[:, h * LIST_COLS : (h + 1) * LIST_COLS]),
+            )
+
+        round_pairs(nc.scalar.copy, 0, 0, 0, HALF_T)
+        round_pairs(nc.vector.tensor_copy, 0, 1, 0, HALF_T)
+        for h in range(2):
+            gather_pairs(0, h)
+        round_pairs(nc.scalar.copy, 1, 0, 0, HALF_T)
+        round_pairs(nc.vector.tensor_copy, 1, 1, 0, VECTOR_SHARE)
+        round_pairs(nc.scalar.copy, 1, 1, VECTOR_SHARE, HALF_T)
+        for h in range(2):
+            gather_pairs(1, h)
+
+        products = {}
+        for h in range(2):
+            x_codes = sb.tile([P, HALF_S], U32, name=f"x_codes{h}", align_bytes=64)
+            x_scales = sb.tile([P, HALF_S], U8, name=f"x_scales{h}", align_bytes=64)
+            nc.vector.quantize_mx(out=x_codes[:].bitcast(FP8X4), scales=x_scales[:], in_=picked[h][:].bitcast(BF16))
+            for b in range(N // P):
+                acc = psum.tile([P, HALF_S], F32, name=f"acc{h}{b}")
+                nc.tensor.matmul_mx(
+                    out=acc[:],
+                    lhsT=w_codes[:, b * P : (b + 1) * P].bitcast(FP8X4),
+                    lhsT_scale=w_scales[:, b * P : (b + 1) * P],
+                    rhs=x_codes[:].bitcast(FP8X4),
+                    rhs_scale=x_scales[:],
+                    start=True,
+                    stop=True,
+                )
+                products[h, b] = sb.tile([P, HALF_S], F32, name=f"product{h}{b}")
+                nc.scalar.copy(products[h, b][:], acc[:])
+
+        for h in range(2):
+            for b in range(N // P):
+                nc.vector.tensor_tensor(
+                    placed[b][:].indirect(offsets[:, h * LIST_COLS : (h + 1) * LIST_COLS]),
+                    products[h, b][:],
+                    scores[:, h * HALF_S : (h + 1) * HALF_S],
+                    MULT,
+                )
+        for b in range(N // P):
+            nc.sync.dma_start(out[b * P : (b + 1) * P, :], placed[b][:])

@@ -19,9 +19,7 @@ MULT = mybir.AluOpType.mult
 P = 128
 PACK = 4
 HALF_T = T // 2
-HALF_S = S // 2
-LIST_COLS = HALF_S // 16
-GATE_ROW = T // P
+PIECES = ((0, 128), (128, 256), (256, 512))
 VECTOR_SHARE = 352
 
 
@@ -31,10 +29,14 @@ def tile_picked_modgate_linnone_l_kernel(tc, xT, gate, w1_words, w1_scales, offs
         sb = ctx.enter_context(tc.tile_pool(name="sb", bufs=1))
         psum = ctx.enter_context(tc.psum_pool(name="psum", bufs=1))
 
-        gate_cols = sb.tile([P, GATE_ROW], F32, name="gate_cols")
-        nc.sync.dma_start(gate_cols[:], gate[0, :].rearrange("(n m) -> n m", m=GATE_ROW))
         offsets = sb.tile([P, S // 16], U16, name="offsets")
         nc.sync.dma_start(offsets[:], offs)
+        gate_row = sb.tile([P, T], F32, name="gate_row")
+        nc.sync.dma_start(gate_row[P - 1 : P, :], gate[0:1, :])
+        nc.vector.memset(gate_row[0 : P - 1, :], 0.0)
+
+        def entries(lo, hi):
+            return offsets[:, lo // 16 : hi // 16]
 
         x_rows = xT.rearrange("(p j) t -> p j t", j=PACK)
         raw = {}
@@ -46,27 +48,28 @@ def tile_picked_modgate_linnone_l_kernel(tc, xT, gate, w1_words, w1_scales, offs
         w_codes = sb.tile([P, N], U32, name="w_codes", align_bytes=64)
         nc.sync.dma_start(w_codes[:].bitcast(I32), w1_words[0].rearrange("p n t -> p (n t)").bitcast(I32))
         w_scales = sb.tile([P, N], U8, name="w_scales", align_bytes=64)
-        nc.vector.memset(w_scales[:].bitcast(I32), 0)
+        nc.gpsimd.memset(w_scales[:].bitcast(I32), 0)
         for q in range(4):
             nc.sync.dma_start(w_scales[32 * q : 32 * q + 4, :].bitcast(I32), w1_scales[0, 4 * q : 4 * q + 4, :].bitcast(I32))
-
-        placed = [sb.tile([P, T], F32, name=f"placed{b}") for b in range(N // P)]
-        for window in placed:
-            nc.vector.memset(window[:], 0.0)
 
         identity = sb.tile([P, P], F32, name="identity")
         make_identity(nc, identity[:])
 
-        gate_all = sb.tile([P, T], F32, name="gate_all")
-        gate_by_m = gate_all[:].rearrange("p (n m) -> p n m", m=GATE_ROW)
-        for half, engine_copy in enumerate((nc.vector.tensor_copy, nc.scalar.copy)):
-            spread = psum.tile([P, 4, P], F32, name=f"spread{half}")
-            for i in range(4):
-                m = 4 * half + i
-                nc.tensor.transpose(spread[:, i, :], gate_cols[:, m : m + 1].to_broadcast([P, P]), identity[:])
-            engine_copy(gate_by_m[:, :, 4 * half : 4 * half + 4], spread[:].rearrange("p m n -> p n m"))
+        placed = [sb.tile([P, T], F32, name=f"placed{b}") for b in range(N // P)]
+        nc.vector.memset(placed[0][:], 0.0)
+        nc.gpsimd.memset(placed[1][:], 0.0)
+
+        score_row = sb.tile([P, S], F32, name="score_row")
+        nc.vector.tensor_copy(score_row[:], gate_row[:].indirect(offsets[:]))
+        turned = psum.tile([P, S // P, P], F32, name="turned")
+        for i in range(S // P):
+            nc.tensor.transpose(turned[:, i, :], score_row[:, i * P : (i + 1) * P], identity[:])
+        score_cols = sb.tile([P, S // P], F32, name="score_cols")
+        nc.scalar.copy(score_cols[:], turned[:, :, P - 1])
+        spread = psum.tile([P, S], F32, name="spread")
+        for i in range(S // P):
+            nc.tensor.transpose(spread[:, i * P : (i + 1) * P], score_cols[:, i : i + 1].to_broadcast([P, P]), identity[:])
         scores = sb.tile([P, S], F32, name="scores")
-        nc.vector.tensor_copy(scores[:], gate_all[:].indirect(offsets[:]))
 
         pairs = [sb.tile([P, T], U32, name=f"pairs{u}") for u in range(2)]
 
@@ -74,31 +77,22 @@ def tile_picked_modgate_linnone_l_kernel(tc, xT, gate, w1_words, w1_scales, offs
             dst = pairs[u][:].bitcast(BF16).rearrange("p (t e) -> p t e", e=2)
             engine_copy(dst[:, c * HALF_T + lo : c * HALF_T + hi, :], raw[u, c][:, :, lo:hi].rearrange("p e t -> p t e"))
 
-        picked = [sb.tile([P, HALF_S * 2], U32, name=f"picked{h}", align_bytes=64) for h in range(2)]
+        picked = [sb.tile([P, 2 * (hi - lo)], U32, name=f"picked{lo}", align_bytes=64) for lo, hi in PIECES]
 
-        def gather_pairs(u, h):
+        def gather_pairs(u, i):
             nc.vector.tensor_copy(
-                picked[h][:].rearrange("p (s u) -> p s u", u=2)[:, :, u],
-                pairs[u][:].indirect(offsets[:, h * LIST_COLS : (h + 1) * LIST_COLS]),
+                picked[i][:].rearrange("p (s u) -> p s u", u=2)[:, :, u], pairs[u][:].indirect(entries(*PIECES[i]))
             )
 
-        round_pairs(nc.scalar.copy, 0, 0, 0, HALF_T)
-        round_pairs(nc.vector.tensor_copy, 0, 1, 0, HALF_T)
-        for h in range(2):
-            gather_pairs(0, h)
-        round_pairs(nc.scalar.copy, 1, 0, 0, HALF_T)
-        round_pairs(nc.vector.tensor_copy, 1, 1, 0, VECTOR_SHARE)
-        round_pairs(nc.scalar.copy, 1, 1, VECTOR_SHARE, HALF_T)
-        for h in range(2):
-            gather_pairs(1, h)
-
         products = {}
-        for h in range(2):
-            x_codes = sb.tile([P, HALF_S], U32, name=f"x_codes{h}", align_bytes=64)
-            x_scales = sb.tile([P, HALF_S], U8, name=f"x_scales{h}", align_bytes=64)
-            nc.vector.quantize_mx(out=x_codes[:].bitcast(FP8X4), scales=x_scales[:], in_=picked[h][:].bitcast(BF16))
+
+        def multiply(i):
+            width = PIECES[i][1] - PIECES[i][0]
+            x_codes = sb.tile([P, width], U32, name=f"x_codes{i}", align_bytes=64)
+            x_scales = sb.tile([P, width], U8, name=f"x_scales{i}", align_bytes=64)
+            nc.vector.quantize_mx(out=x_codes[:].bitcast(FP8X4), scales=x_scales[:], in_=picked[i][:].bitcast(BF16))
             for b in range(N // P):
-                acc = psum.tile([P, HALF_S], F32, name=f"acc{h}{b}")
+                acc = psum.tile([P, width], F32, name=f"acc{i}{b}")
                 nc.tensor.matmul_mx(
                     out=acc[:],
                     lhsT=w_codes[:, b * P : (b + 1) * P].bitcast(FP8X4),
@@ -108,16 +102,25 @@ def tile_picked_modgate_linnone_l_kernel(tc, xT, gate, w1_words, w1_scales, offs
                     start=True,
                     stop=True,
                 )
-                products[h, b] = sb.tile([P, HALF_S], F32, name=f"product{h}{b}")
-                nc.scalar.copy(products[h, b][:], acc[:])
+                products[i, b] = sb.tile([P, width], F32, name=f"product{i}{b}")
+                nc.scalar.copy(products[i, b][:], acc[:])
 
-        for h in range(2):
+        round_pairs(nc.scalar.copy, 0, 0, 0, HALF_T)
+        round_pairs(nc.vector.tensor_copy, 0, 1, 0, HALF_T)
+        nc.scalar.copy(scores[:], spread[:])
+        for i in range(len(PIECES)):
+            gather_pairs(0, i)
+        round_pairs(nc.scalar.copy, 1, 0, 0, HALF_T)
+        round_pairs(nc.vector.tensor_copy, 1, 1, 0, VECTOR_SHARE)
+        round_pairs(nc.scalar.copy, 1, 1, VECTOR_SHARE, HALF_T)
+        gather_pairs(1, 0)
+        for i in range(len(PIECES)):
+            if i + 1 < len(PIECES):
+                gather_pairs(1, i + 1)
+            multiply(i)
+
+        for i, (lo, hi) in enumerate(PIECES):
             for b in range(N // P):
-                nc.vector.tensor_tensor(
-                    placed[b][:].indirect(offsets[:, h * LIST_COLS : (h + 1) * LIST_COLS]),
-                    products[h, b][:],
-                    scores[:, h * HALF_S : (h + 1) * HALF_S],
-                    MULT,
-                )
+                nc.vector.tensor_tensor(placed[b][:].indirect(entries(lo, hi)), products[i, b][:], scores[:, lo:hi], MULT)
         for b in range(N // P):
             nc.sync.dma_start(out[b * P : (b + 1) * P, :], placed[b][:])

@@ -84,7 +84,7 @@ def tile_picked_modgate_linnone_l_kernel(tc, xT, gate, w1_words, w1_scales, offs
                 picked[i][:].rearrange("p (s u) -> p s u", u=2)[:, :, u], pairs[u][:].indirect(entries(*PIECES[i]))
             )
 
-        products = {}
+        products = [sb.tile([P, S], F32, name=f"products{b}") for b in range(N // P)]
 
         def multiply(i):
             width = PIECES[i][1] - PIECES[i][0]
@@ -102,11 +102,11 @@ def tile_picked_modgate_linnone_l_kernel(tc, xT, gate, w1_words, w1_scales, offs
                     start=True,
                     stop=True,
                 )
-                products[i, b] = sb.tile([P, width], F32, name=f"product{i}{b}")
-                nc.scalar.copy(products[i, b][:], acc[:])
+                nc.scalar.copy(products[b][:, slice(*PIECES[i])], acc[:])
 
         round_pairs(nc.scalar.copy, 0, 0, 0, HALF_T)
-        round_pairs(nc.vector.tensor_copy, 0, 1, 0, HALF_T)
+        round_pairs(nc.vector.tensor_copy, 0, 1, 0, VECTOR_SHARE)
+        round_pairs(nc.scalar.copy, 0, 1, VECTOR_SHARE, HALF_T)
         nc.scalar.copy(scores[:], spread[:])
         for i in range(len(PIECES)):
             gather_pairs(0, i)
@@ -119,8 +119,8 @@ def tile_picked_modgate_linnone_l_kernel(tc, xT, gate, w1_words, w1_scales, offs
                 gather_pairs(1, i + 1)
             multiply(i)
 
-        for i, (lo, hi) in enumerate(PIECES):
+        for lo, hi in ((0, 128), (128, 512)):
             for b in range(N // P):
-                nc.vector.tensor_tensor(placed[b][:].indirect(entries(lo, hi)), products[i, b][:], scores[:, lo:hi], MULT)
+                nc.vector.tensor_tensor(placed[b][:].indirect(entries(lo, hi)), products[b][:, lo:hi], scores[:, lo:hi], MULT)
         for b in range(N // P):
             nc.sync.dma_start(out[b * P : (b + 1) * P, :], placed[b][:])

@@ -59,11 +59,16 @@ def tile_picked_modgate_linnone_l_kernel(tc, xT, gate, w1_words, w1_scales, offs
         nc.vector.memset(placed[0][:], 0.0)
         nc.gpsimd.memset(placed[1][:], 0.0)
 
-        score_row = sb.tile([P, S], F32, name="score_row")
-        nc.vector.tensor_copy(score_row[:], gate_row[:].indirect(offsets[:]))
+        pairs = [sb.tile([P, T], U32, name=f"pairs{u}") for u in range(2)]
+        score_head = sb.tile([P, S - P], F32, name="score_head")
         turned = psum.tile([P, S // P, P], F32, name="turned")
         for i in range(S // P):
-            nc.tensor.transpose(turned[:, i, :], score_row[:, i * P : (i + 1) * P], identity[:])
+            if i + 1 < S // P:
+                chunk = score_head[:, i * P : (i + 1) * P]
+            else:
+                chunk = pairs[1][:, HALF_T - P // 2 : HALF_T + P // 2].bitcast(F32)
+            nc.vector.tensor_copy(chunk, gate_row[:].indirect(entries(i * P, (i + 1) * P)))
+            nc.tensor.transpose(turned[:, i, :], chunk, identity[:])
         score_cols = sb.tile([P, S // P], F32, name="score_cols")
         nc.scalar.copy(score_cols[:], turned[:, :, P - 1])
         spread = psum.tile([P, S], F32, name="spread")
@@ -71,56 +76,84 @@ def tile_picked_modgate_linnone_l_kernel(tc, xT, gate, w1_words, w1_scales, offs
             nc.tensor.transpose(spread[:, i * P : (i + 1) * P], score_cols[:, i : i + 1].to_broadcast([P, P]), identity[:])
         scores = sb.tile([P, S], F32, name="scores")
 
-        pairs = [sb.tile([P, T], U32, name=f"pairs{u}") for u in range(2)]
-
         def round_pairs(engine_copy, u, c, lo, hi):
             dst = pairs[u][:].bitcast(BF16).rearrange("p (t e) -> p t e", e=2)
             engine_copy(dst[:, c * HALF_T + lo : c * HALF_T + hi, :], raw[u, c][:, :, lo:hi].rearrange("p e t -> p t e"))
 
-        picked = [sb.tile([P, 2 * (hi - lo)], U32, name=f"picked{lo}", align_bytes=64) for lo, hi in PIECES]
+        def width(i):
+            return PIECES[i][1] - PIECES[i][0]
+
+        loose = sb.tile([P, 2 * width(2)], U32, name="loose", tag="p10", align_bytes=64)
+        picked = {0: loose[:, width(2) :], 1: sb.tile([P, 2 * width(1)], U32, name="picked1", align_bytes=64)[:]}
 
         def gather_pairs(u, i):
-            nc.vector.tensor_copy(
-                picked[i][:].rearrange("p (s u) -> p s u", u=2)[:, :, u], pairs[u][:].indirect(entries(*PIECES[i]))
+            if i == 2:
+                dst = loose[:, u * width(2) : (u + 1) * width(2)]
+            else:
+                dst = picked[i].rearrange("p (s u) -> p s u", u=2)[:, :, u]
+            nc.vector.tensor_copy(dst, pairs[u][:].indirect(entries(*PIECES[i])))
+
+        x_codes, x_scales, products = {}, {}, {}
+
+        def quantise(i, tag):
+            x_codes[i] = sb.tile([P, width(i)], U32, name=f"x_codes{i}", align_bytes=64)
+            x_scales[i] = sb.tile([P, width(i)], U8, name=f"x_scales{i}", tag=tag, align_bytes=64)
+            nc.vector.quantize_mx(out=x_codes[i][:].bitcast(FP8X4), scales=x_scales[i][:], in_=picked[i].bitcast(BF16))
+
+        def product(i, b, acc):
+            nc.tensor.matmul_mx(
+                out=acc,
+                lhsT=w_codes[:, b * P : (b + 1) * P].bitcast(FP8X4),
+                lhsT_scale=w_scales[:, b * P : (b + 1) * P],
+                rhs=x_codes[i][:].bitcast(FP8X4),
+                rhs_scale=x_scales[i][:],
+                start=True,
+                stop=True,
             )
 
-        products = [sb.tile([P, S], F32, name=f"products{b}") for b in range(N // P)]
-
         def multiply(i):
-            width = PIECES[i][1] - PIECES[i][0]
-            x_codes = sb.tile([P, width], U32, name=f"x_codes{i}", align_bytes=64)
-            x_scales = sb.tile([P, width], U8, name=f"x_scales{i}", align_bytes=64)
-            nc.vector.quantize_mx(out=x_codes[:].bitcast(FP8X4), scales=x_scales[:], in_=picked[i][:].bitcast(BF16))
             for b in range(N // P):
-                acc = psum.tile([P, width], F32, name=f"acc{i}{b}")
-                nc.tensor.matmul_mx(
-                    out=acc[:],
-                    lhsT=w_codes[:, b * P : (b + 1) * P].bitcast(FP8X4),
-                    lhsT_scale=w_scales[:, b * P : (b + 1) * P],
-                    rhs=x_codes[:].bitcast(FP8X4),
-                    rhs_scale=x_scales[:],
-                    start=True,
-                    stop=True,
+                acc = psum.tile([P, width(i)], F32, name=f"acc{i}{b}")
+                product(i, b, acc[:])
+                products[i, b] = sb.tile([P, width(i)], F32, name=f"products{i}{b}", tag=f"p{i}{b}", align_bytes=64)[:]
+                nc.scalar.copy(products[i, b], acc[:])
+
+        def multiply_together(i):
+            acc = psum.tile([P, N // P, width(i)], F32, name=f"acc{i}")
+            both = sb.tile([P, N // P, width(i)], F32, name=f"products{i}", tag=f"p{i}0", align_bytes=64)
+            for b in range(N // P):
+                product(i, b, acc[:, b, :])
+                products[i, b] = both[:, b, :]
+            nc.scalar.copy(both[:], acc[:])
+
+        def scatter(i):
+            for b in range(N // P):
+                nc.vector.tensor_tensor(
+                    placed[b][:].indirect(entries(*PIECES[i])), products[i, b], scores[:, slice(*PIECES[i])], MULT
                 )
-                nc.scalar.copy(products[b][:, slice(*PIECES[i])], acc[:])
 
         round_pairs(nc.scalar.copy, 0, 0, 0, HALF_T)
         round_pairs(nc.vector.tensor_copy, 0, 1, 0, VECTOR_SHARE)
         round_pairs(nc.scalar.copy, 0, 1, VECTOR_SHARE, HALF_T)
-        nc.scalar.copy(scores[:], spread[:])
         for i in range(len(PIECES)):
             gather_pairs(0, i)
         round_pairs(nc.scalar.copy, 1, 0, 0, HALF_T)
-        round_pairs(nc.vector.tensor_copy, 1, 1, 0, VECTOR_SHARE)
-        round_pairs(nc.scalar.copy, 1, 1, VECTOR_SHARE, HALF_T)
+        round_pairs(nc.vector.tensor_copy, 1, 1, HALF_T - VECTOR_SHARE, HALF_T)
+        round_pairs(nc.scalar.copy, 1, 1, 0, HALF_T - VECTOR_SHARE)
+        nc.scalar.copy(scores[:], spread[:])
         gather_pairs(1, 0)
-        for i in range(len(PIECES)):
-            if i + 1 < len(PIECES):
-                gather_pairs(1, i + 1)
-            multiply(i)
-
-        for lo, hi in ((0, 128), (128, 512)):
-            for b in range(N // P):
-                nc.vector.tensor_tensor(placed[b][:].indirect(entries(lo, hi)), products[b][:, lo:hi], scores[:, lo:hi], MULT)
+        gather_pairs(1, 1)
+        quantise(0, "xs0")
+        quantise(1, "xs1")
+        gather_pairs(1, 2)
+        multiply(0)
+        picked[2] = sb.tile([P, 2 * width(2)], U32, name="picked2", tag="xs0", align_bytes=64)[:]
+        nc.scalar.copy(picked[2].rearrange("p (s u) -> p s u", u=2), loose[:].rearrange("p (u s) -> p s u", u=2))
+        multiply_together(1)
+        scatter(0)
+        quantise(2, "p00")
+        multiply(2)
+        scatter(1)
+        scatter(2)
         for b in range(N // P):
             nc.sync.dma_start(out[b * P : (b + 1) * P, :], placed[b][:])

@@ -32,7 +32,7 @@ def tile_picked_modgate_linnone_l_kernel(tc, xT, gate, w1_words, w1_scales, offs
         offsets = sb.tile([P, S // 16], U16, name="offsets")
         nc.sync.dma_start(offsets[:], offs)
         gate_row = sb.tile([P, T], F32, name="gate_row")
-        nc.sync.dma_start(gate_row[P - 1 : P, :], gate[0:1, :])
+        nc.scalar.dma_start(gate_row[P - 1 : P, :], gate[0:1, :])
         nc.vector.memset(gate_row[0 : P - 1, :], 0.0)
 
         def entries(lo, hi):
@@ -50,7 +50,7 @@ def tile_picked_modgate_linnone_l_kernel(tc, xT, gate, w1_words, w1_scales, offs
         w_scales = sb.tile([P, N], U8, name="w_scales", align_bytes=64)
         nc.gpsimd.memset(w_scales[:].bitcast(I32), 0)
         for q in range(4):
-            nc.sync.dma_start(w_scales[32 * q : 32 * q + 4, :].bitcast(I32), w1_scales[0, 4 * q : 4 * q + 4, :].bitcast(I32))
+            nc.scalar.dma_start(w_scales[32 * q : 32 * q + 4, :].bitcast(I32), w1_scales[0, 4 * q : 4 * q + 4, :].bitcast(I32))
 
         identity = sb.tile([P, P], F32, name="identity")
         make_identity(nc, identity[:])

@@ -83,15 +83,22 @@ def tile_picked_modgate_linnone_l_kernel(tc, xT, gate, w1_words, w1_scales, offs
         def width(i):
             return PIECES[i][1] - PIECES[i][0]
 
-        loose = sb.tile([P, 2 * width(2)], U32, name="loose", tag="p10", align_bytes=64)
-        picked = {0: loose[:, width(2) :], 1: sb.tile([P, 2 * width(1)], U32, name="picked1", align_bytes=64)[:]}
+        rest = S - width(0)
+        loose = sb.tile([P, 2 * rest], U32, name="loose", tag="p10", align_bytes=64)
+        picked = {0: loose[:, 2 * rest - 2 * width(0) :]}
 
-        def gather_pairs(u, i):
-            if i == 2:
-                dst = loose[:, u * width(2) : (u + 1) * width(2)]
-            else:
-                dst = picked[i].rearrange("p (s u) -> p s u", u=2)[:, :, u]
-            nc.vector.tensor_copy(dst, pairs[u][:].indirect(entries(*PIECES[i])))
+        def gather_first(u):
+            dst = picked[0].rearrange("p (s u) -> p s u", u=2)[:, :, u]
+            nc.vector.tensor_copy(dst, pairs[u][:].indirect(entries(*PIECES[0])))
+
+        def gather_loose(u, lo, hi):
+            start = u * rest - width(0)
+            nc.vector.tensor_copy(loose[:, start + lo : start + hi], pairs[u][:].indirect(entries(lo, hi)))
+
+        def weave(i, tag):
+            picked[i] = sb.tile([P, 2 * width(i)], U32, name=f"picked{i}", tag=tag, align_bytes=64)[:]
+            lo, hi = PIECES[i][0] - width(0), PIECES[i][1] - width(0)
+            nc.scalar.copy(picked[i].rearrange("p (s u) -> p s u", u=2), loose[:].rearrange("p (u s) -> p s u", u=2)[:, lo:hi, :])
 
         x_codes, x_scales, products = {}, {}, {}
 
@@ -135,20 +142,20 @@ def tile_picked_modgate_linnone_l_kernel(tc, xT, gate, w1_words, w1_scales, offs
         round_pairs(nc.scalar.copy, 0, 0, 0, HALF_T)
         round_pairs(nc.vector.tensor_copy, 0, 1, 0, VECTOR_SHARE)
         round_pairs(nc.scalar.copy, 0, 1, VECTOR_SHARE, HALF_T)
-        for i in range(len(PIECES)):
-            gather_pairs(0, i)
+        gather_first(0)
+        gather_loose(0, width(0), S)
         round_pairs(nc.scalar.copy, 1, 0, 0, HALF_T)
         round_pairs(nc.vector.tensor_copy, 1, 1, HALF_T - VECTOR_SHARE, HALF_T)
         round_pairs(nc.scalar.copy, 1, 1, 0, HALF_T - VECTOR_SHARE)
         nc.scalar.copy(scores[:], spread[:])
-        gather_pairs(1, 0)
-        gather_pairs(1, 1)
+        gather_first(1)
+        gather_loose(1, *PIECES[1])
         quantise(0, "xs0")
+        weave(1, "picked1")
         quantise(1, "xs1")
-        gather_pairs(1, 2)
+        gather_loose(1, *PIECES[2])
         multiply(0)
-        picked[2] = sb.tile([P, 2 * width(2)], U32, name="picked2", tag="xs0", align_bytes=64)[:]
-        nc.scalar.copy(picked[2].rearrange("p (s u) -> p s u", u=2), loose[:].rearrange("p (u s) -> p s u", u=2))
+        weave(2, "xs0")
         multiply_together(1)
         scatter(0)
         quantise(2, "p00")

@@ -20,7 +20,10 @@ P = 128
 PACK = 4
 HALF_T = T // 2
 PIECES = ((0, 128), (128, 256), (256, 512))
-VECTOR_SHARE = 352
+EDGE = 160
+LAST_CUTS = (0, 160, 320, 512)
+SPARE = 8
+LEAD = 16
 
 
 def tile_picked_modgate_linnone_l_kernel(tc, xT, gate, w1_words, w1_scales, offs, out):
@@ -39,11 +42,18 @@ def tile_picked_modgate_linnone_l_kernel(tc, xT, gate, w1_words, w1_scales, offs
             return offsets[:, lo // 16 : hi // 16]
 
         x_rows = xT.rearrange("(p j) t -> p j t", j=PACK)
-        raw = {}
-        for u in range(2):
-            for c in range(2):
-                raw[u, c] = sb.tile([P, 2, HALF_T], F32, name=f"raw{u}{c}")
-                nc.sync.dma_start(raw[u, c][:], x_rows[:, 2 * u : 2 * u + 2, c * HALF_T : (c + 1) * HALF_T])
+        stage = sb.tile([P, LEAD + 2 * T], F32, name="stage", align_bytes=64)
+        pairs = stage[:, LEAD : LEAD + T]
+        picked = stage[:, LEAD + T : LEAD + 2 * T]
+        plane3 = sb.tile([P, T + S], F32, name="plane3")
+        scores = plane3[:, T : T + S]
+        plane2 = sb.tile([P, T], F32, name="plane2")
+        nc.sync.dma_start(plane2[:], x_rows[:, 2, :])
+        raw_hi = sb.tile([P, 2, HALF_T], F32, name="raw_hi")
+        nc.sync.dma_start(raw_hi[:], x_rows[:, 0:2, HALF_T:T])
+        raw_lo = sb.tile([P, 2, HALF_T], F32, name="raw_lo", tag="late", align_bytes=64)
+        nc.sync.dma_start(raw_lo[:], x_rows[:, 0:2, 0:HALF_T])
+        nc.sync.dma_start(plane3[:, 0:T], x_rows[:, 3, :])
 
         w_codes = sb.tile([P, N], U32, name="w_codes", align_bytes=64)
         nc.sync.dma_start(w_codes[:].bitcast(I32), w1_words[0].rearrange("p n t -> p (n t)").bitcast(I32))
@@ -59,53 +69,38 @@ def tile_picked_modgate_linnone_l_kernel(tc, xT, gate, w1_words, w1_scales, offs
         nc.vector.memset(placed[0][:], 0.0)
         nc.gpsimd.memset(placed[1][:], 0.0)
 
-        pairs = [sb.tile([P, T], U32, name=f"pairs{u}") for u in range(2)]
+        rounded2 = sb.tile([P, T], BF16, name="rounded2")
+        nc.scalar.copy(rounded2[:], plane2[:])
+
         score_head = sb.tile([P, S - P], F32, name="score_head")
         turned = psum.tile([P, S // P, P], F32, name="turned")
         for i in range(S // P):
             if i + 1 < S // P:
                 chunk = score_head[:, i * P : (i + 1) * P]
             else:
-                chunk = pairs[1][:, HALF_T - P // 2 : HALF_T + P // 2].bitcast(F32)
+                chunk = picked[:, T - P : T]
             nc.vector.tensor_copy(chunk, gate_row[:].indirect(entries(i * P, (i + 1) * P)))
             nc.tensor.transpose(turned[:, i, :], chunk, identity[:])
-        score_cols = sb.tile([P, S // P], F32, name="score_cols")
-        nc.scalar.copy(score_cols[:], turned[:, :, P - 1])
+        score_cols = stage[:, LEAD - 3 : LEAD + 1]
+        nc.scalar.copy(score_cols, turned[:, :, P - 1])
         spread = psum.tile([P, S], F32, name="spread")
-        for i in range(S // P):
+        for i in reversed(range(S // P)):
             nc.tensor.transpose(spread[:, i * P : (i + 1) * P], score_cols[:, i : i + 1].to_broadcast([P, P]), identity[:])
-        scores = sb.tile([P, S], F32, name="scores")
 
-        def round_pairs(engine_copy, u, c, lo, hi):
-            dst = pairs[u][:].bitcast(BF16).rearrange("p (t e) -> p t e", e=2)
-            engine_copy(dst[:, c * HALF_T + lo : c * HALF_T + hi, :], raw[u, c][:, :, lo:hi].rearrange("p e t -> p t e"))
+        pair_values = pairs.bitcast(BF16).rearrange("p (t e) -> p t e", e=2)
+        picked_values = picked.bitcast(BF16).rearrange("p (s j) -> p s j", j=PACK)
+        picked_words = picked.bitcast(U32).rearrange("p (s u) -> p s u", u=2)
 
         def width(i):
             return PIECES[i][1] - PIECES[i][0]
 
-        rest = S - width(0)
-        loose = sb.tile([P, 2 * rest], U32, name="loose", tag="p10", align_bytes=64)
-        picked = {0: loose[:, 2 * rest - 2 * width(0) :]}
-
-        def gather_first(u):
-            dst = picked[0].rearrange("p (s u) -> p s u", u=2)[:, :, u]
-            nc.vector.tensor_copy(dst, pairs[u][:].indirect(entries(*PIECES[0])))
-
-        def gather_loose(u, lo, hi):
-            start = u * rest - width(0)
-            nc.vector.tensor_copy(loose[:, start + lo : start + hi], pairs[u][:].indirect(entries(lo, hi)))
-
-        def weave(i, tag):
-            picked[i] = sb.tile([P, 2 * width(i)], U32, name=f"picked{i}", tag=tag, align_bytes=64)[:]
-            lo, hi = PIECES[i][0] - width(0), PIECES[i][1] - width(0)
-            nc.scalar.copy(picked[i].rearrange("p (s u) -> p s u", u=2), loose[:].rearrange("p (u s) -> p s u", u=2)[:, lo:hi, :])
-
         x_codes, x_scales, products = {}, {}, {}
 
-        def quantise(i, tag):
+        def quantise(i):
             x_codes[i] = sb.tile([P, width(i)], U32, name=f"x_codes{i}", align_bytes=64)
-            x_scales[i] = sb.tile([P, width(i)], U8, name=f"x_scales{i}", tag=tag, align_bytes=64)
-            nc.vector.quantize_mx(out=x_codes[i][:].bitcast(FP8X4), scales=x_scales[i][:], in_=picked[i].bitcast(BF16))
+            x_scales[i] = sb.tile([P, width(i)], U8, name=f"x_scales{i}", align_bytes=64)[:]
+            lo, hi = PIECES[i]
+            nc.vector.quantize_mx(out=x_codes[i][:].bitcast(FP8X4), scales=x_scales[i], in_=picked[:, 2 * lo : 2 * hi].bitcast(BF16))
 
         def product(i, b, acc):
             nc.tensor.matmul_mx(
@@ -113,25 +108,19 @@ def tile_picked_modgate_linnone_l_kernel(tc, xT, gate, w1_words, w1_scales, offs
                 lhsT=w_codes[:, b * P : (b + 1) * P].bitcast(FP8X4),
                 lhsT_scale=w_scales[:, b * P : (b + 1) * P],
                 rhs=x_codes[i][:].bitcast(FP8X4),
-                rhs_scale=x_scales[i][:],
+                rhs_scale=x_scales[i],
                 start=True,
                 stop=True,
             )
 
-        def multiply(i):
-            for b in range(N // P):
-                acc = psum.tile([P, width(i)], F32, name=f"acc{i}{b}")
-                product(i, b, acc[:])
-                products[i, b] = sb.tile([P, width(i)], F32, name=f"products{i}{b}", tag=f"p{i}{b}", align_bytes=64)[:]
-                nc.scalar.copy(products[i, b], acc[:])
+        def multiply(i, b, dst):
+            acc = psum.tile([P, width(i)], F32, name=f"acc{i}{b}")
+            product(i, b, acc[:])
+            products[i, b] = dst
+            nc.scalar.copy(dst, acc[:])
 
-        def multiply_together(i):
-            acc = psum.tile([P, N // P, width(i)], F32, name=f"acc{i}")
-            both = sb.tile([P, N // P, width(i)], F32, name=f"products{i}", tag=f"p{i}0", align_bytes=64)
-            for b in range(N // P):
-                product(i, b, acc[:, b, :])
-                products[i, b] = both[:, b, :]
-            nc.scalar.copy(both[:], acc[:])
+        def own(i, b):
+            return sb.tile([P, width(i)], F32, name=f"products{i}{b}")[:]
 
         def scatter(i):
             for b in range(N // P):
@@ -139,27 +128,42 @@ def tile_picked_modgate_linnone_l_kernel(tc, xT, gate, w1_words, w1_scales, offs
                     placed[b][:].indirect(entries(*PIECES[i])), products[i, b], scores[:, slice(*PIECES[i])], MULT
                 )
 
-        round_pairs(nc.scalar.copy, 0, 0, 0, HALF_T)
-        round_pairs(nc.vector.tensor_copy, 0, 1, 0, VECTOR_SHARE)
-        round_pairs(nc.scalar.copy, 0, 1, VECTOR_SHARE, HALF_T)
-        gather_first(0)
-        gather_loose(0, width(0), S)
-        round_pairs(nc.scalar.copy, 1, 0, 0, HALF_T)
-        round_pairs(nc.vector.tensor_copy, 1, 1, HALF_T - VECTOR_SHARE, HALF_T)
-        round_pairs(nc.scalar.copy, 1, 1, 0, HALF_T - VECTOR_SHARE)
-        nc.scalar.copy(scores[:], spread[:])
-        gather_first(1)
-        gather_loose(1, *PIECES[1])
-        quantise(0, "xs0")
-        weave(1, "picked1")
-        quantise(1, "xs1")
-        gather_loose(1, *PIECES[2])
-        multiply(0)
-        weave(2, "xs0")
-        multiply_together(1)
+        def gather_rounded(j, rounded):
+            nc.scalar.activation(
+                picked_values[:, LAST_CUTS[2] : S, j],
+                rounded[:].indirect(entries(LAST_CUTS[2], S)),
+                mybir.ActivationFunctionType.Copy,
+            )
+
+        nc.vector.tensor_copy(picked_values[:, 0 : LAST_CUTS[2], 2], plane2[:].indirect(entries(0, LAST_CUTS[2])))
+        gather_rounded(2, rounded2)
+        nc.vector.tensor_copy(pair_values[:, HALF_T:T, :], raw_hi[:].rearrange("p e t -> p t e"))
+        nc.vector.tensor_copy(pair_values[:, EDGE:HALF_T, :], raw_lo[:, :, EDGE:HALF_T].rearrange("p e t -> p t e"))
+        nc.scalar.copy(pair_values[:, 0:EDGE, :], raw_lo[:, :, 0:EDGE].rearrange("p e t -> p t e"))
+        nc.scalar.copy(scores, spread[:])
+        nc.vector.tensor_copy(picked_words[:, 0 : PIECES[1][1], 0], pairs.bitcast(U32).indirect(entries(0, PIECES[1][1])))
+
+        rounded3 = sb.tile([P, T], BF16, name="rounded3", tag="late", align_bytes=64)
+        nc.scalar.copy(rounded3[:], plane3[:, 0:T])
+        gather_rounded(3, rounded3)
+        for c in range(2):
+            lo, hi = LAST_CUTS[c], LAST_CUTS[c + 1]
+            nc.vector.tensor_copy(picked_values[:, lo:hi, 3], plane3[:, 0 : T + SPARE].indirect(entries(lo, hi)))
+        quantise(0)
+        nc.vector.tensor_copy(picked_words[:, PIECES[2][0] : S, 0], stage[:, LEAD : LEAD + T + SPARE].bitcast(U32).indirect(entries(*PIECES[2])))
+        quantise(1)
+        multiply(0, 0, own(0, 0))
+        multiply(0, 1, own(0, 1))
+        acc1 = psum.tile([P, N // P, width(1)], F32, name="acc1")
+        both = sb.tile([P, N // P, width(1)], F32, name="both")
+        for b in range(N // P):
+            product(1, b, acc1[:, b, :])
+            products[1, b] = both[:, b, :]
+        nc.scalar.copy(both[:], acc1[:])
         scatter(0)
-        quantise(2, "p00")
-        multiply(2)
+        quantise(2)
+        multiply(2, 0, own(2, 0))
+        multiply(2, 1, own(2, 1))
         scatter(1)
         scatter(2)
         for b in range(N // P):

@@ -23,7 +23,10 @@ PIECES = ((0, 128), (128, 256), (256, 512))
 EDGE = 160
 LAST_CUTS = (0, 160, 320, 512)
 SPARE = 8
+PAIR_CUT = 288
 LEAD = 16
+PAD = 16
+STRIP = 48
 
 
 def tile_picked_modgate_linnone_l_kernel(tc, xT, gate, w1_words, w1_scales, offs, out):
@@ -45,7 +48,8 @@ def tile_picked_modgate_linnone_l_kernel(tc, xT, gate, w1_words, w1_scales, offs
         stage = sb.tile([P, LEAD + 2 * T], F32, name="stage", align_bytes=64)
         pairs = stage[:, LEAD : LEAD + T]
         picked = stage[:, LEAD + T : LEAD + 2 * T]
-        plane3 = sb.tile([P, T + S], F32, name="plane3")
+        lead3 = sb.tile([P, P + T + S], F32, name="lead3")
+        plane3 = lead3[:, P:]
         scores = plane3[:, T : T + S]
         plane2 = sb.tile([P, T], F32, name="plane2")
         nc.sync.dma_start(plane2[:], x_rows[:, 2, :])
@@ -131,35 +135,38 @@ def tile_picked_modgate_linnone_l_kernel(tc, xT, gate, w1_words, w1_scales, offs
         def gather_rounded(j, rounded):
             nc.scalar.activation(
                 picked_values[:, LAST_CUTS[2] : S, j],
-                rounded[:].indirect(entries(LAST_CUTS[2], S)),
+                rounded.indirect(entries(LAST_CUTS[2], S)),
                 mybir.ActivationFunctionType.Copy,
             )
 
         nc.vector.tensor_copy(picked_values[:, 0 : LAST_CUTS[2], 2], plane2[:].indirect(entries(0, LAST_CUTS[2])))
-        gather_rounded(2, rounded2)
+        gather_rounded(2, rounded2[:])
         nc.vector.tensor_copy(pair_values[:, HALF_T:T, :], raw_hi[:].rearrange("p e t -> p t e"))
         nc.vector.tensor_copy(pair_values[:, EDGE:HALF_T, :], raw_lo[:, :, EDGE:HALF_T].rearrange("p e t -> p t e"))
         nc.scalar.copy(pair_values[:, 0:EDGE, :], raw_lo[:, :, 0:EDGE].rearrange("p e t -> p t e"))
-        nc.scalar.copy(scores, spread[:])
-        nc.vector.tensor_copy(picked_words[:, 0 : PIECES[1][1], 0], pairs.bitcast(U32).indirect(entries(0, PIECES[1][1])))
+        nc.scalar.copy(scores[:, 0:P], spread[:, 0:P])
+        nc.scalar.copy(scores[:, P:S], spread[:, P:S])
+        nc.vector.tensor_copy(picked_words[:, 0:P, 0], pairs.bitcast(U32).indirect(entries(*PIECES[0])))
 
-        rounded3 = sb.tile([P, T], BF16, name="rounded3", tag="late", align_bytes=64)
-        nc.scalar.copy(rounded3[:], plane3[:, 0:T])
-        gather_rounded(3, rounded3)
+        late = sb.tile([P, PAD + T], BF16, name="late", tag="late", align_bytes=64)
+        nc.scalar.copy(late[:, PAD + STRIP :], plane3[:, STRIP:T])
         for c in range(2):
             lo, hi = LAST_CUTS[c], LAST_CUTS[c + 1]
             nc.vector.tensor_copy(picked_values[:, lo:hi, 3], plane3[:, 0 : T + SPARE].indirect(entries(lo, hi)))
         quantise(0)
-        nc.vector.tensor_copy(picked_words[:, PIECES[2][0] : S, 0], stage[:, LEAD : LEAD + T + SPARE].bitcast(U32).indirect(entries(*PIECES[2])))
+        for lo, hi in ((P, PAIR_CUT), (PAIR_CUT, S)):
+            nc.vector.tensor_copy(picked_words[:, lo:hi, 0], stage[:, LEAD : LEAD + T + SPARE].bitcast(U32).indirect(entries(lo, hi)))
         quantise(1)
-        multiply(0, 0, own(0, 0))
+        multiply(0, 0, lead3[:, 0:P])
         multiply(0, 1, own(0, 1))
+        nc.scalar.copy(late[:, 0 : PAD + STRIP], lead3[:, P - PAD : P + STRIP])
+        gather_rounded(3, late[:, PAD:])
         acc1 = psum.tile([P, N // P, width(1)], F32, name="acc1")
-        both = sb.tile([P, N // P, width(1)], F32, name="both")
+        both = late[:, PAD : PAD + 4 * P].bitcast(F32)
         for b in range(N // P):
             product(1, b, acc1[:, b, :])
-            products[1, b] = both[:, b, :]
-        nc.scalar.copy(both[:], acc1[:])
+            products[1, b] = both[:, b * P : (b + 1) * P]
+        nc.scalar.copy(both, acc1[:].rearrange("p b s -> p (b s)"))
         scatter(0)
         quantise(2)
         multiply(2, 0, own(2, 0))

@@ -15,18 +15,12 @@ U16 = mybir.dt.uint16
 U8 = mybir.dt.uint8
 FP8X4 = mybir.dt.float8_e4m3fn_x4
 MULT = mybir.AluOpType.mult
+COPY = mybir.ActivationFunctionType.Copy
 
 P = 128
 PACK = 4
-HALF_T = T // 2
 PIECES = ((0, 128), (128, 256), (256, 512))
-EDGE = 160
-LAST_CUTS = (0, 160, 320, 512)
-SPARE = 8
-PAIR_CUT = 288
-LEAD = 16
-PAD = 16
-STRIP = 48
+HALF = 256
 
 
 def tile_picked_modgate_linnone_l_kernel(tc, xT, gate, w1_words, w1_scales, offs, out):
@@ -37,6 +31,8 @@ def tile_picked_modgate_linnone_l_kernel(tc, xT, gate, w1_words, w1_scales, offs
 
         offsets = sb.tile([P, S // 16], U16, name="offsets")
         nc.sync.dma_start(offsets[:], offs)
+        placed = [sb.tile([P, T], F32, name=f"placed{b}") for b in range(N // P)]
+        nc.vector.memset(placed[0][:], 0.0)
         gate_row = sb.tile([P, T], F32, name="gate_row")
         nc.scalar.dma_start(gate_row[P - 1 : P, :], gate[0:1, :])
         nc.vector.memset(gate_row[0 : P - 1, :], 0.0)
@@ -45,133 +41,126 @@ def tile_picked_modgate_linnone_l_kernel(tc, xT, gate, w1_words, w1_scales, offs
             return offsets[:, lo // 16 : hi // 16]
 
         x_rows = xT.rearrange("(p j) t -> p j t", j=PACK)
-        stage = sb.tile([P, LEAD + 2 * T], F32, name="stage", align_bytes=64)
-        pairs = stage[:, LEAD : LEAD + T]
-        picked = stage[:, LEAD + T : LEAD + 2 * T]
-        lead3 = sb.tile([P, P + T + S], F32, name="lead3")
-        plane3 = lead3[:, P:]
-        scores = plane3[:, T : T + S]
-        plane2 = sb.tile([P, T], F32, name="plane2")
-        nc.sync.dma_start(plane2[:], x_rows[:, 2, :])
-        raw_hi = sb.tile([P, 2, HALF_T], F32, name="raw_hi")
-        nc.sync.dma_start(raw_hi[:], x_rows[:, 0:2, HALF_T:T])
-        raw_lo = sb.tile([P, 2, HALF_T], F32, name="raw_lo", tag="late", align_bytes=64)
-        nc.sync.dma_start(raw_lo[:], x_rows[:, 0:2, 0:HALF_T])
-        nc.sync.dma_start(plane3[:, 0:T], x_rows[:, 3, :])
+        tails = (S, 4, 0, 0)
+        planes = [sb.tile([P, T + tails[j]], F32, name=f"plane{j}") for j in range(PACK)]
+        for j in range(PACK):
+            nc.sync.dma_start(planes[j][:, 0:T], x_rows[:, j, :])
+        woven_a = sb.tile([P, HALF * PACK], BF16, name="woven_a", align_bytes=64)
+        score_halves = [woven_a[:, 0 : 2 * HALF].bitcast(F32), woven_a[:, 2 * HALF : 4 * HALF].bitcast(F32)]
+
+        def scores(lo, hi):
+            return score_halves[lo // HALF][:, lo % HALF : lo % HALF + hi - lo]
 
         w_codes = sb.tile([P, N], U32, name="w_codes", align_bytes=64)
         nc.sync.dma_start(w_codes[:].bitcast(I32), w1_words[0].rearrange("p n t -> p (n t)").bitcast(I32))
         w_scales = sb.tile([P, N], U8, name="w_scales", align_bytes=64)
         nc.gpsimd.memset(w_scales[:].bitcast(I32), 0)
         for q in range(4):
-            nc.scalar.dma_start(w_scales[32 * q : 32 * q + 4, :].bitcast(I32), w1_scales[0, 4 * q : 4 * q + 4, :].bitcast(I32))
+            nc.sync.dma_start(w_scales[32 * q : 32 * q + 4, :].bitcast(I32), w1_scales[0, 4 * q : 4 * q + 4, :].bitcast(I32))
 
         identity = sb.tile([P, P], F32, name="identity")
         make_identity(nc, identity[:])
 
-        placed = [sb.tile([P, T], F32, name=f"placed{b}") for b in range(N // P)]
-        nc.vector.memset(placed[0][:], 0.0)
-        nc.gpsimd.memset(placed[1][:], 0.0)
+        nc.scalar.copy(placed[1][:, 0 : T // 2], placed[0][:, 0 : T // 2])
+        nc.gpsimd.memset(placed[1][:, T // 2 : T], 0.0)
 
-        rounded2 = sb.tile([P, T], BF16, name="rounded2")
-        nc.scalar.copy(rounded2[:], plane2[:])
-
-        score_head = sb.tile([P, S - P], F32, name="score_head")
         turned = psum.tile([P, S // P, P], F32, name="turned")
-        for i in range(S // P):
-            if i + 1 < S // P:
-                chunk = score_head[:, i * P : (i + 1) * P]
+        chunks = planes[0][:, T:]
+        for c in (0, 2, 1, 3):
+            cols = slice(c * P, (c + 1) * P)
+            if c < 2:
+                nc.vector.tensor_copy(chunks[:, cols], gate_row[:].indirect(entries(c * P, (c + 1) * P)))
             else:
-                chunk = picked[:, T - P : T]
-            nc.vector.tensor_copy(chunk, gate_row[:].indirect(entries(i * P, (i + 1) * P)))
-            nc.tensor.transpose(turned[:, i, :], chunk, identity[:])
-        score_cols = stage[:, LEAD - 3 : LEAD + 1]
-        nc.scalar.copy(score_cols, turned[:, :, P - 1])
-        spread = psum.tile([P, S], F32, name="spread")
-        for i in reversed(range(S // P)):
-            nc.tensor.transpose(spread[:, i * P : (i + 1) * P], score_cols[:, i : i + 1].to_broadcast([P, P]), identity[:])
+                nc.scalar.activation(chunks[:, cols], gate_row[:].indirect(entries(c * P, (c + 1) * P)), COPY)
+            nc.tensor.transpose(turned[:, c, :], chunks[:, cols], identity[:])
+        score_cols = planes[1][:, T:]
 
-        pair_values = pairs.bitcast(BF16).rearrange("p (t e) -> p t e", e=2)
-        picked_values = picked.bitcast(BF16).rearrange("p (s j) -> p s j", j=PACK)
-        picked_words = picked.bitcast(U32).rearrange("p (s u) -> p s u", u=2)
+        woven_b = sb.tile([P, (S - HALF) * PACK], BF16, name="woven_b", align_bytes=64)
+        values_a = woven_a[:].rearrange("p (s j) -> p s j", j=PACK)
+        values_b = woven_b[:].rearrange("p (s j) -> p s j", j=PACK)
+        flat = sb.tile([P, 2 * (S - HALF)], BF16, name="flat")
+
+        def gather_a(j, lo, hi):
+            nc.vector.tensor_copy(values_a[:, lo:hi, j], planes[j][:, 0 : (T if j == 1 else T + tails[j])].indirect(entries(lo, hi)))
+
+        def gather_b(j, lo, hi):
+            base = (j % 2) * (S - HALF) - HALF
+            nc.scalar.activation(flat[:, base + lo : base + hi], planes[j][:].indirect(entries(lo, hi)), COPY)
+
+        def weave(u, lo, hi):
+            src = flat[:].rearrange("p (e s) -> p s e", e=2)
+            nc.scalar.copy(values_b[:, lo - HALF : hi - HALF, 2 * u : 2 * u + 2], src[:, lo - HALF : hi - HALF, :])
 
         def width(i):
             return PIECES[i][1] - PIECES[i][0]
 
-        x_codes, x_scales, products = {}, {}, {}
+        x_codes, x_scales, acc = {}, {}, {}
 
-        def quantise(i):
+        def quantise(i, src):
             x_codes[i] = sb.tile([P, width(i)], U32, name=f"x_codes{i}", align_bytes=64)
-            x_scales[i] = sb.tile([P, width(i)], U8, name=f"x_scales{i}", align_bytes=64)[:]
-            lo, hi = PIECES[i]
-            nc.vector.quantize_mx(out=x_codes[i][:].bitcast(FP8X4), scales=x_scales[i], in_=picked[:, 2 * lo : 2 * hi].bitcast(BF16))
-
-        def product(i, b, acc):
-            nc.tensor.matmul_mx(
-                out=acc,
-                lhsT=w_codes[:, b * P : (b + 1) * P].bitcast(FP8X4),
-                lhsT_scale=w_scales[:, b * P : (b + 1) * P],
-                rhs=x_codes[i][:].bitcast(FP8X4),
-                rhs_scale=x_scales[i],
-                start=True,
-                stop=True,
-            )
-
-        def multiply(i, b, dst):
-            acc = psum.tile([P, width(i)], F32, name=f"acc{i}{b}")
-            product(i, b, acc[:])
-            products[i, b] = dst
-            nc.scalar.copy(dst, acc[:])
-
-        def own(i, b):
-            return sb.tile([P, width(i)], F32, name=f"products{i}{b}")[:]
-
-        def scatter(i):
+            x_scales[i] = sb.tile([P, width(i)], U8, name=f"x_scales{i}", align_bytes=64)
+            nc.vector.quantize_mx(out=x_codes[i][:].bitcast(FP8X4), scales=x_scales[i][:], in_=src)
             for b in range(N // P):
-                nc.vector.tensor_tensor(
-                    placed[b][:].indirect(entries(*PIECES[i])), products[i, b], scores[:, slice(*PIECES[i])], MULT
+                acc[i, b] = psum.tile([P, width(i)], F32, name=f"acc{i}{b}")
+                nc.tensor.matmul_mx(
+                    out=acc[i, b][:],
+                    lhsT=w_codes[:, b * P : (b + 1) * P].bitcast(FP8X4),
+                    lhsT_scale=w_scales[:, b * P : (b + 1) * P],
+                    rhs=x_codes[i][:].bitcast(FP8X4),
+                    rhs_scale=x_scales[i][:],
+                    start=True,
+                    stop=True,
                 )
 
-        def gather_rounded(j, rounded):
-            nc.scalar.activation(
-                picked_values[:, LAST_CUTS[2] : S, j],
-                rounded.indirect(entries(LAST_CUTS[2], S)),
-                mybir.ActivationFunctionType.Copy,
-            )
+        weighted = [sb.tile([P, S - P], F32, name=f"weighted{b}") for b in range(N // P)]
+        firsts = flat[:].bitcast(F32)
 
-        nc.vector.tensor_copy(picked_values[:, 0 : LAST_CUTS[2], 2], plane2[:].indirect(entries(0, LAST_CUTS[2])))
-        gather_rounded(2, rounded2[:])
-        nc.vector.tensor_copy(pair_values[:, HALF_T:T, :], raw_hi[:].rearrange("p e t -> p t e"))
-        nc.vector.tensor_copy(pair_values[:, EDGE:HALF_T, :], raw_lo[:, :, EDGE:HALF_T].rearrange("p e t -> p t e"))
-        nc.scalar.copy(pair_values[:, 0:EDGE, :], raw_lo[:, :, 0:EDGE].rearrange("p e t -> p t e"))
-        nc.scalar.copy(scores[:, 0:P], spread[:, 0:P])
-        nc.scalar.copy(scores[:, P:S], spread[:, P:S])
-        nc.vector.tensor_copy(picked_words[:, 0:P, 0], pairs.bitcast(U32).indirect(entries(*PIECES[0])))
+        def products(i, b):
+            if i == 0:
+                return firsts[:, b * P : (b + 1) * P]
+            return weighted[b][:, PIECES[i][0] - P : PIECES[i][1] - P]
 
-        late = sb.tile([P, PAD + T], BF16, name="late", tag="late", align_bytes=64)
-        nc.scalar.copy(late[:, PAD + STRIP :], plane3[:, STRIP:T])
-        for c in range(2):
-            lo, hi = LAST_CUTS[c], LAST_CUTS[c + 1]
-            nc.vector.tensor_copy(picked_values[:, lo:hi, 3], plane3[:, 0 : T + SPARE].indirect(entries(lo, hi)))
-        quantise(0)
-        for lo, hi in ((P, PAIR_CUT), (PAIR_CUT, S)):
-            nc.vector.tensor_copy(picked_words[:, lo:hi, 0], stage[:, LEAD : LEAD + T + SPARE].bitcast(U32).indirect(entries(lo, hi)))
-        quantise(1)
-        multiply(0, 0, lead3[:, 0:P])
-        multiply(0, 1, own(0, 1))
-        nc.scalar.copy(late[:, 0 : PAD + STRIP], lead3[:, P - PAD : P + STRIP])
-        gather_rounded(3, late[:, PAD:])
-        acc1 = psum.tile([P, N // P, width(1)], F32, name="acc1")
-        both = late[:, PAD : PAD + 4 * P].bitcast(F32)
-        for b in range(N // P):
-            product(1, b, acc1[:, b, :])
-            products[1, b] = both[:, b * P : (b + 1) * P]
-        nc.scalar.copy(both, acc1[:].rearrange("p b s -> p (b s)"))
-        scatter(0)
-        quantise(2)
-        multiply(2, 0, own(2, 0))
-        multiply(2, 1, own(2, 1))
-        scatter(1)
-        scatter(2)
+        def weigh(i, b):
+            nc.vector.tensor_tensor(products(i, b), acc[i, b][:], scores(*PIECES[i]), MULT)
+
+        def scatter_first(i):
+            nc.scalar.activation(placed[0][:].indirect(entries(*PIECES[i])), products(i, 0), COPY)
+
+        gather_a(0, 0, HALF)
+        gather_b(0, HALF, S)
+        nc.scalar.copy(score_cols, turned[:, :, P - 1])
+        spread = psum.tile([P, S], F32, name="spread")
+        for i in range(S // P):
+            nc.tensor.transpose(spread[:, i * P : (i + 1) * P], score_cols[:, i : i + 1].to_broadcast([P, P]), identity[:])
+        gather_a(1, 0, HALF)
+        for lo in (HALF, HALF + P):
+            gather_b(1, lo, lo + P)
+        for lo in (HALF, HALF + P):
+            weave(0, lo, lo + P)
+        gather_a(2, 0, HALF)
+        for lo in (HALF, HALF + P):
+            gather_b(2, lo, lo + P)
+        gather_a(3, 0, P)
+        gather_a(3, P, HALF)
+        gather_b(3, HALF, HALF + P)
+        gather_b(3, HALF + P, S)
+        weave(1, HALF, HALF + P)
+        weave(1, HALF + P, S)
+        quantise(0, woven_a[:, 0 : PACK * P])
+        quantise(1, woven_a[:, PACK * P : PACK * HALF])
+        nc.vector.tensor_copy(scores(0, HALF), spread[:, 0:HALF])
+        nc.vector.tensor_copy(scores(HALF, S), spread[:, HALF:S])
+        weigh(0, 0)
+        nc.scalar.copy(products(0, 1), acc[0, 1][:])
+        scatter_first(0)
+        quantise(2, woven_b[:])
+        weigh(1, 0)
+        scatter_first(1)
+        nc.vector.tensor_tensor(placed[1][:].indirect(entries(0, P)), products(0, 1), scores(0, P), MULT)
+        weigh(2, 0)
+        scatter_first(2)
+        weigh(1, 1)
+        weigh(2, 1)
+        nc.vector.tensor_copy(placed[1][:].indirect(entries(P, S)), weighted[1][:])
         for b in range(N // P):
             nc.sync.dma_start(out[b * P : (b + 1) * P, :], placed[b][:])

@@ -40,11 +40,16 @@ def tile_picked_modgate_linnone_l_kernel(tc, xT, gate, w1_words, w1_scales, offs
         def entries(lo, hi):
             return offsets[:, lo // 16 : hi // 16]
 
+        w_scales = sb.tile([P, N], U8, name="w_scales", align_bytes=64)
+        nc.gpsimd.memset(w_scales[:].bitcast(I32), 0)
         x_rows = xT.rearrange("(p j) t -> p j t", j=PACK)
         tails = (S, 4, 0, 0)
         planes = [sb.tile([P, T + tails[j]], F32, name=f"plane{j}") for j in range(PACK)]
         for j in range(PACK):
             nc.sync.dma_start(planes[j][:, 0:T], x_rows[:, j, :])
+            if j == 1:
+                for q in range(4):
+                    nc.sync.dma_start(w_scales[32 * q : 32 * q + 4, :].bitcast(I32), w1_scales[0, 4 * q : 4 * q + 4, :].bitcast(I32))
         woven_a = sb.tile([P, HALF * PACK], BF16, name="woven_a", align_bytes=64)
         score_halves = [woven_a[:, 0 : 2 * HALF].bitcast(F32), woven_a[:, 2 * HALF : 4 * HALF].bitcast(F32)]
 
@@ -53,10 +58,6 @@ def tile_picked_modgate_linnone_l_kernel(tc, xT, gate, w1_words, w1_scales, offs
 
         w_codes = sb.tile([P, N], U32, name="w_codes", align_bytes=64)
         nc.sync.dma_start(w_codes[:].bitcast(I32), w1_words[0].rearrange("p n t -> p (n t)").bitcast(I32))
-        w_scales = sb.tile([P, N], U8, name="w_scales", align_bytes=64)
-        nc.gpsimd.memset(w_scales[:].bitcast(I32), 0)
-        for q in range(4):
-            nc.sync.dma_start(w_scales[32 * q : 32 * q + 4, :].bitcast(I32), w1_scales[0, 4 * q : 4 * q + 4, :].bitcast(I32))
 
         identity = sb.tile([P, P], F32, name="identity")
         make_identity(nc, identity[:])

@@ -21,6 +21,7 @@ P = 128
 PACK = 4
 PIECES = ((0, 128), (128, 256), (256, 512))
 HALF = 256
+CUTS = ((256, 384, 512), (256, 384, 512))
 
 
 def tile_picked_modgate_linnone_l_kernel(tc, xT, gate, w1_words, w1_scales, offs, out):
@@ -31,8 +32,8 @@ def tile_picked_modgate_linnone_l_kernel(tc, xT, gate, w1_words, w1_scales, offs
 
         offsets = sb.tile([P, S // 16], U16, name="offsets")
         nc.sync.dma_start(offsets[:], offs)
-        placed = [sb.tile([P, T], F32, name=f"placed{b}") for b in range(N // P)]
-        nc.vector.memset(placed[0][:], 0.0)
+        placed = [sb.tile([P, T + (HALF if b == 0 else 0)], F32, name=f"placed{b}") for b in range(N // P)]
+        nc.vector.memset(placed[0][:, 0:T], 0.0)
         gate_row = sb.tile([P, T], F32, name="gate_row")
         nc.scalar.dma_start(gate_row[P - 1 : P, :], gate[0:1, :])
         nc.vector.memset(gate_row[0 : P - 1, :], 0.0)
@@ -50,11 +51,6 @@ def tile_picked_modgate_linnone_l_kernel(tc, xT, gate, w1_words, w1_scales, offs
             if j == 1:
                 for q in range(4):
                     nc.sync.dma_start(w_scales[32 * q : 32 * q + 4, :].bitcast(I32), w1_scales[0, 4 * q : 4 * q + 4, :].bitcast(I32))
-        woven_a = sb.tile([P, HALF * PACK], BF16, name="woven_a", align_bytes=64)
-        score_halves = [woven_a[:, 0 : 2 * HALF].bitcast(F32), woven_a[:, 2 * HALF : 4 * HALF].bitcast(F32)]
-
-        def scores(lo, hi):
-            return score_halves[lo // HALF][:, lo % HALF : lo % HALF + hi - lo]
 
         w_codes = sb.tile([P, N], U32, name="w_codes", align_bytes=64)
         nc.sync.dma_start(w_codes[:].bitcast(I32), w1_words[0].rearrange("p n t -> p (n t)").bitcast(I32))
@@ -76,21 +72,24 @@ def tile_picked_modgate_linnone_l_kernel(tc, xT, gate, w1_words, w1_scales, offs
             nc.tensor.transpose(turned[:, c, :], chunks[:, cols], identity[:])
         score_cols = planes[1][:, T:]
 
-        woven_b = sb.tile([P, (S - HALF) * PACK], BF16, name="woven_b", align_bytes=64)
-        values_a = woven_a[:].rearrange("p (s j) -> p s j", j=PACK)
-        values_b = woven_b[:].rearrange("p (s j) -> p s j", j=PACK)
-        flat = sb.tile([P, 2 * (S - HALF)], BF16, name="flat")
+        woven = sb.tile([P, S * PACK], BF16, name="woven", align_bytes=64)
+        values = woven[:].rearrange("p (s j) -> p s j", j=PACK)
+        scores = woven[:, 0 : 2 * S].bitcast(F32)
+        flat = placed[0][:, T:].bitcast(BF16)
+        flat_pairs = flat.rearrange("p (e s) -> p s e", e=2)
 
         def gather_a(j, lo, hi):
-            nc.vector.tensor_copy(values_a[:, lo:hi, j], planes[j][:, 0 : (T if j == 1 else T + tails[j])].indirect(entries(lo, hi)))
+            nc.vector.tensor_copy(values[:, lo:hi, j], planes[j][:, 0 : (T + S if j == 0 else T)].indirect(entries(lo, hi)))
 
-        def gather_b(j, lo, hi):
-            base = (j % 2) * (S - HALF) - HALF
-            nc.scalar.activation(flat[:, base + lo : base + hi], planes[j][:].indirect(entries(lo, hi)), COPY)
+        def gather_b(j):
+            base = (j % 2) * HALF - HALF
+            cuts = CUTS[j // 2]
+            for lo, hi in zip(cuts, cuts[1:]):
+                nc.scalar.activation(flat[:, base + lo : base + hi], planes[j][:].indirect(entries(lo, hi)), COPY)
 
-        def weave(u, lo, hi):
-            src = flat[:].rearrange("p (e s) -> p s e", e=2)
-            nc.scalar.copy(values_b[:, lo - HALF : hi - HALF, 2 * u : 2 * u + 2], src[:, lo - HALF : hi - HALF, :])
+        def weave(u):
+            for lo, hi in zip(CUTS[u], CUTS[u][1:]):
+                nc.scalar.copy(values[:, lo:hi, 2 * u : 2 * u + 2], flat_pairs[:, lo - HALF : hi - HALF, :])
 
         def width(i):
             return PIECES[i][1] - PIECES[i][0]
@@ -113,55 +112,48 @@ def tile_picked_modgate_linnone_l_kernel(tc, xT, gate, w1_words, w1_scales, offs
                     stop=True,
                 )
 
-        weighted = [sb.tile([P, S - P], F32, name=f"weighted{b}") for b in range(N // P)]
-        firsts = flat[:].bitcast(F32)
-
-        def products(i, b):
-            if i == 0:
-                return firsts[:, b * P : (b + 1) * P]
-            return weighted[b][:, PIECES[i][0] - P : PIECES[i][1] - P]
+        weighted = [sb.tile([P, S], F32, name=f"weighted{b}") for b in range(N // P)]
 
         def weigh(i, b):
-            nc.vector.tensor_tensor(products(i, b), acc[i, b][:], scores(*PIECES[i]), MULT)
+            cols = slice(*PIECES[i])
+            nc.vector.tensor_tensor(weighted[b][:, cols], acc[i, b][:], scores[:, cols], MULT)
 
-        def scatter_first(i):
-            nc.scalar.activation(placed[0][:].indirect(entries(*PIECES[i])), products(i, 0), COPY)
+        def scatter_first(lo, hi):
+            nc.scalar.activation(placed[0][:].indirect(entries(lo, hi)), weighted[0][:, lo:hi], COPY)
 
-        gather_a(0, 0, HALF)
-        gather_b(0, HALF, S)
+        def scatter_second(lo, hi):
+            nc.vector.tensor_copy(placed[1][:].indirect(entries(lo, hi)), weighted[1][:, lo:hi])
+
+        gather_a(0, 0, CUTS[0][0])
+        gather_b(0)
         nc.scalar.copy(score_cols, turned[:, :, P - 1])
         spread = psum.tile([P, S], F32, name="spread")
         for i in range(S // P):
             nc.tensor.transpose(spread[:, i * P : (i + 1) * P], score_cols[:, i : i + 1].to_broadcast([P, P]), identity[:])
-        gather_a(1, 0, HALF)
-        for lo in (HALF, HALF + P):
-            gather_b(1, lo, lo + P)
-        for lo in (HALF, HALF + P):
-            weave(0, lo, lo + P)
-        gather_a(2, 0, HALF)
-        for lo in (HALF, HALF + P):
-            gather_b(2, lo, lo + P)
+        gather_a(1, 0, CUTS[0][0])
+        gather_b(1)
+        weave(0)
+        gather_a(2, 0, CUTS[1][0])
+        gather_b(2)
         gather_a(3, 0, P)
-        gather_a(3, P, HALF)
-        gather_b(3, HALF, HALF + P)
-        gather_b(3, HALF + P, S)
-        weave(1, HALF, HALF + P)
-        weave(1, HALF + P, S)
-        quantise(0, woven_a[:, 0 : PACK * P])
-        quantise(1, woven_a[:, PACK * P : PACK * HALF])
-        nc.vector.tensor_copy(scores(0, HALF), spread[:, 0:HALF])
-        nc.vector.tensor_copy(scores(HALF, S), spread[:, HALF:S])
+        gather_a(3, P, CUTS[1][0])
+        gather_b(3)
+        weave(1)
+        for i in range(2):
+            quantise(i, woven[:, PACK * PIECES[i][0] : PACK * PIECES[i][1]])
+        for lo in (0, HALF):
+            nc.vector.tensor_copy(scores[:, lo : lo + HALF], spread[:, lo : lo + HALF])
         weigh(0, 0)
-        nc.scalar.copy(products(0, 1), acc[0, 1][:])
-        scatter_first(0)
-        quantise(2, woven_b[:])
         weigh(1, 0)
-        scatter_first(1)
-        nc.vector.tensor_tensor(placed[1][:].indirect(entries(0, P)), products(0, 1), scores(0, P), MULT)
-        weigh(2, 0)
-        scatter_first(2)
+        quantise(2, woven[:, PACK * HALF :])
+        plain = planes[3][:, 0:P]
+        nc.scalar.copy(plain, acc[0, 1][:])
+        scatter_first(0, HALF)
         weigh(1, 1)
+        nc.vector.tensor_tensor(placed[1][:].indirect(entries(0, P)), plain, scores[:, 0:P], MULT)
+        weigh(2, 0)
         weigh(2, 1)
-        nc.vector.tensor_copy(placed[1][:].indirect(entries(P, S)), weighted[1][:])
+        scatter_first(HALF, S)
+        scatter_second(P, S)
         for b in range(N // P):
-            nc.sync.dma_start(out[b * P : (b + 1) * P, :], placed[b][:])
+            nc.sync.dma_start(out[b * P : (b + 1) * P, :], placed[b][:, 0:T])

@@ -19,9 +19,8 @@ COPY = mybir.ActivationFunctionType.Copy
 
 P = 128
 PACK = 4
-PIECES = ((0, 128), (128, 256), (256, 512))
 HALF = 256
-CUTS = ((256, 384, 512), (256, 384, 512))
+CUTS = ((320, 416, 512), (256, 384, 512))
 
 
 def tile_picked_modgate_linnone_l_kernel(tc, xT, gate, w1_words, w1_scales, offs, out):
@@ -44,7 +43,7 @@ def tile_picked_modgate_linnone_l_kernel(tc, xT, gate, w1_words, w1_scales, offs
         w_scales = sb.tile([P, N], U8, name="w_scales", align_bytes=64)
         nc.gpsimd.memset(w_scales[:].bitcast(I32), 0)
         x_rows = xT.rearrange("(p j) t -> p j t", j=PACK)
-        tails = (S, 4, 0, 0)
+        tails = (S, 4, 0, HALF)
         planes = [sb.tile([P, T + tails[j]], F32, name=f"plane{j}") for j in range(PACK)]
         for j in range(PACK):
             nc.sync.dma_start(planes[j][:, 0:T], x_rows[:, j, :])
@@ -74,7 +73,11 @@ def tile_picked_modgate_linnone_l_kernel(tc, xT, gate, w1_words, w1_scales, offs
 
         woven = sb.tile([P, S * PACK], BF16, name="woven", align_bytes=64)
         values = woven[:].rearrange("p (s j) -> p s j", j=PACK)
-        scores = woven[:, 0 : 2 * S].bitcast(F32)
+        score_halves = (planes[3][:, T:], woven[:, 0:S].bitcast(F32))
+
+        def scores(lo, hi):
+            return score_halves[lo // HALF][:, lo % HALF : lo % HALF + hi - lo]
+
         flat = placed[0][:, T:].bitcast(BF16)
         flat_pairs = flat.rearrange("p (e s) -> p s e", e=2)
 
@@ -91,38 +94,34 @@ def tile_picked_modgate_linnone_l_kernel(tc, xT, gate, w1_words, w1_scales, offs
             for lo, hi in zip(CUTS[u], CUTS[u][1:]):
                 nc.scalar.copy(values[:, lo:hi, 2 * u : 2 * u + 2], flat_pairs[:, lo - HALF : hi - HALF, :])
 
-        def width(i):
-            return PIECES[i][1] - PIECES[i][0]
+        x_codes = sb.tile([P, S], U32, name="x_codes", align_bytes=64)
+        x_scales = sb.tile([P, S], U8, name="x_scales", align_bytes=64)
 
-        x_codes, x_scales, acc = {}, {}, {}
+        def quantise(lo, hi):
+            nc.vector.quantize_mx(out=x_codes[:, lo:hi].bitcast(FP8X4), scales=x_scales[:, lo:hi], in_=woven[:, PACK * lo : PACK * hi])
 
-        def quantise(i, src):
-            x_codes[i] = sb.tile([P, width(i)], U32, name=f"x_codes{i}", align_bytes=64)
-            x_scales[i] = sb.tile([P, width(i)], U8, name=f"x_scales{i}", align_bytes=64)
-            nc.vector.quantize_mx(out=x_codes[i][:].bitcast(FP8X4), scales=x_scales[i][:], in_=src)
-            for b in range(N // P):
-                acc[i, b] = psum.tile([P, width(i)], F32, name=f"acc{i}{b}")
-                nc.tensor.matmul_mx(
-                    out=acc[i, b][:],
-                    lhsT=w_codes[:, b * P : (b + 1) * P].bitcast(FP8X4),
-                    lhsT_scale=w_scales[:, b * P : (b + 1) * P],
-                    rhs=x_codes[i][:].bitcast(FP8X4),
-                    rhs_scale=x_scales[i][:],
-                    start=True,
-                    stop=True,
-                )
+        def multiply(b, lo, hi):
+            acc = psum.tile([P, hi - lo], F32, name=f"acc{b}_{lo}")
+            nc.tensor.matmul_mx(
+                out=acc[:],
+                lhsT=w_codes[:, b * P : (b + 1) * P].bitcast(FP8X4),
+                lhsT_scale=w_scales[:, b * P : (b + 1) * P],
+                rhs=x_codes[:, lo:hi].bitcast(FP8X4),
+                rhs_scale=x_scales[:, lo:hi],
+                start=True,
+                stop=True,
+            )
+            return acc[:]
 
-        weighted = [sb.tile([P, S], F32, name=f"weighted{b}") for b in range(N // P)]
+        weighted = sb.tile([P, S], F32, name="weighted")
+        plain = planes[3][:, 0:P]
+        weighted_rest = sb.tile([P, S - P], F32, name="weighted_rest")
 
-        def weigh(i, b):
-            cols = slice(*PIECES[i])
-            nc.vector.tensor_tensor(weighted[b][:, cols], acc[i, b][:], scores[:, cols], MULT)
+        def weigh(lo, hi):
+            nc.vector.tensor_tensor(weighted[:, lo:hi], multiply(0, lo, hi), scores(lo, hi), MULT)
 
         def scatter_first(lo, hi):
-            nc.scalar.activation(placed[0][:].indirect(entries(lo, hi)), weighted[0][:, lo:hi], COPY)
-
-        def scatter_second(lo, hi):
-            nc.vector.tensor_copy(placed[1][:].indirect(entries(lo, hi)), weighted[1][:, lo:hi])
+            nc.scalar.activation(placed[0][:].indirect(entries(lo, hi)), weighted[:, lo:hi], COPY)
 
         gather_a(0, 0, CUTS[0][0])
         gather_b(0)
@@ -133,27 +132,27 @@ def tile_picked_modgate_linnone_l_kernel(tc, xT, gate, w1_words, w1_scales, offs
         gather_a(1, 0, CUTS[0][0])
         gather_b(1)
         weave(0)
+        nc.scalar.copy(scores(0, HALF), spread[:, 0:HALF])
         gather_a(2, 0, CUTS[1][0])
         gather_b(2)
         gather_a(3, 0, P)
         gather_a(3, P, CUTS[1][0])
         gather_b(3)
         weave(1)
-        for i in range(2):
-            quantise(i, woven[:, PACK * PIECES[i][0] : PACK * PIECES[i][1]])
-        for lo in (0, HALF):
-            nc.vector.tensor_copy(scores[:, lo : lo + HALF], spread[:, lo : lo + HALF])
-        weigh(0, 0)
-        weigh(1, 0)
-        quantise(2, woven[:, PACK * HALF :])
-        plain = planes[3][:, 0:P]
-        nc.scalar.copy(plain, acc[0, 1][:])
+        for lo in (0, P):
+            quantise(lo, lo + P)
+        nc.vector.tensor_copy(scores(HALF, S), spread[:, HALF:S])
+        for lo in (0, P):
+            weigh(lo, lo + P)
+        quantise(HALF, S)
+        head = multiply(1, 0, HALF)
+        nc.scalar.copy(plain, head[:, 0:P])
         scatter_first(0, HALF)
-        weigh(1, 1)
-        nc.vector.tensor_tensor(placed[1][:].indirect(entries(0, P)), plain, scores[:, 0:P], MULT)
-        weigh(2, 0)
-        weigh(2, 1)
+        nc.vector.tensor_tensor(weighted_rest[:, 0:P], head[:, P:HALF], scores(P, HALF), MULT)
+        nc.vector.tensor_tensor(placed[1][:].indirect(entries(0, P)), plain, scores(0, P), MULT)
+        weigh(HALF, S)
+        nc.vector.tensor_tensor(weighted_rest[:, P:], multiply(1, HALF, S), scores(HALF, S), MULT)
         scatter_first(HALF, S)
-        scatter_second(P, S)
+        nc.vector.tensor_copy(placed[1][:].indirect(entries(P, S)), weighted_rest[:])
         for b in range(N // P):
             nc.sync.dma_start(out[b * P : (b + 1) * P, :], placed[b][:, 0:T])

@@ -31,8 +31,8 @@ def tile_picked_modgate_linnone_l_kernel(tc, xT, gate, w1_words, w1_scales, offs
 
         offsets = sb.tile([P, S // 16], U16, name="offsets")
         nc.sync.dma_start(offsets[:], offs)
-        placed = [sb.tile([P, T + (HALF if b == 0 else 0)], F32, name=f"placed{b}") for b in range(N // P)]
-        nc.vector.memset(placed[0][:, 0:T], 0.0)
+        placed = [sb.tile([P, T], F32, name=f"placed{b}") for b in range(N // P)]
+        nc.vector.memset(placed[0][:], 0.0)
         gate_row = sb.tile([P, T], F32, name="gate_row")
         nc.scalar.dma_start(gate_row[P - 1 : P, :], gate[0:1, :])
         nc.vector.memset(gate_row[0 : P - 1, :], 0.0)
@@ -73,26 +73,28 @@ def tile_picked_modgate_linnone_l_kernel(tc, xT, gate, w1_words, w1_scales, offs
 
         woven = sb.tile([P, S * PACK], BF16, name="woven", align_bytes=64)
         values = woven[:].rearrange("p (s j) -> p s j", j=PACK)
-        score_halves = (planes[3][:, T:], woven[:, 0:S].bitcast(F32))
+        score_halves = (planes[3][:, T:], planes[3][:, P : P + HALF])
 
         def scores(lo, hi):
             return score_halves[lo // HALF][:, lo % HALF : lo % HALF + hi - lo]
 
-        flat = placed[0][:, T:].bitcast(BF16)
-        flat_pairs = flat.rearrange("p (e s) -> p s e", e=2)
+        weighted = sb.tile([P, S], F32, name="weighted")
+        flat = weighted[:, 0:HALF].bitcast(BF16)
+        flat_pairs = flat.rearrange("p (h e s) -> p h s e", h=2, e=2)
 
         def gather_a(j, lo, hi):
             nc.vector.tensor_copy(values[:, lo:hi, j], planes[j][:, 0 : (T + S if j == 0 else T)].indirect(entries(lo, hi)))
 
         def gather_b(j):
-            base = (j % 2) * HALF - HALF
             cuts = CUTS[j // 2]
-            for lo, hi in zip(cuts, cuts[1:]):
-                nc.scalar.activation(flat[:, base + lo : base + hi], planes[j][:].indirect(entries(lo, hi)), COPY)
+            for h in range(2):
+                base = h * HALF + (j % 2) * P
+                nc.scalar.activation(flat[:, base : base + cuts[h + 1] - cuts[h]], planes[j][:].indirect(entries(cuts[h], cuts[h + 1])), COPY)
 
-        def weave(u):
-            for lo, hi in zip(CUTS[u], CUTS[u][1:]):
-                nc.scalar.copy(values[:, lo:hi, 2 * u : 2 * u + 2], flat_pairs[:, lo - HALF : hi - HALF, :])
+        def weave(u, copy):
+            cuts = CUTS[u]
+            for h in range(2):
+                copy(values[:, cuts[h] : cuts[h + 1], 2 * u : 2 * u + 2], flat_pairs[:, h, 0 : cuts[h + 1] - cuts[h], :])
 
         x_codes = sb.tile([P, S], U32, name="x_codes", align_bytes=64)
         x_scales = sb.tile([P, S], U8, name="x_scales", align_bytes=64)
@@ -113,7 +115,6 @@ def tile_picked_modgate_linnone_l_kernel(tc, xT, gate, w1_words, w1_scales, offs
             )
             return acc[:]
 
-        weighted = sb.tile([P, S], F32, name="weighted")
         plain = planes[3][:, 0:P]
         weighted_rest = sb.tile([P, S - P], F32, name="weighted_rest")
 
@@ -131,17 +132,17 @@ def tile_picked_modgate_linnone_l_kernel(tc, xT, gate, w1_words, w1_scales, offs
             nc.tensor.transpose(spread[:, i * P : (i + 1) * P], score_cols[:, i : i + 1].to_broadcast([P, P]), identity[:])
         gather_a(1, 0, CUTS[0][0])
         gather_b(1)
-        weave(0)
+        weave(0, nc.scalar.copy)
         nc.scalar.copy(scores(0, HALF), spread[:, 0:HALF])
         gather_a(2, 0, CUTS[1][0])
         gather_b(2)
         gather_a(3, 0, P)
         gather_a(3, P, CUTS[1][0])
         gather_b(3)
-        weave(1)
         for lo in (0, P):
             quantise(lo, lo + P)
-        nc.vector.tensor_copy(scores(HALF, S), spread[:, HALF:S])
+        weave(1, nc.vector.tensor_copy)
+        nc.scalar.copy(scores(HALF, S), spread[:, HALF:S])
         for lo in (0, P):
             weigh(lo, lo + P)
         quantise(HALF, S)
@@ -155,4 +156,4 @@ def tile_picked_modgate_linnone_l_kernel(tc, xT, gate, w1_words, w1_scales, offs
         scatter_first(HALF, S)
         nc.vector.tensor_copy(placed[1][:].indirect(entries(P, S)), weighted_rest[:])
         for b in range(N // P):
-            nc.sync.dma_start(out[b * P : (b + 1) * P, :], placed[b][:, 0:T])
+            nc.sync.dma_start(out[b * P : (b + 1) * P, :], placed[b][:])

@@ -20,6 +20,7 @@ COPY = mybir.ActivationFunctionType.Copy
 P = 128
 PACK = 4
 HALF = 256
+STRIP = 64
 CUTS = ((320, 416, 512), (256, 384, 512))
 
 
@@ -57,8 +58,8 @@ def tile_picked_modgate_linnone_l_kernel(tc, xT, gate, w1_words, w1_scales, offs
         identity = sb.tile([P, P], F32, name="identity")
         make_identity(nc, identity[:])
 
-        nc.scalar.copy(placed[1][:, 0 : T // 2], placed[0][:, 0 : T // 2])
-        nc.gpsimd.memset(placed[1][:, T // 2 : T], 0.0)
+        nc.scalar.copy(placed[1][:, 0:STRIP], placed[0][:, 0:STRIP])
+        nc.sync.dma_start(placed[1][:, STRIP:T], placed[0][:, STRIP:T])
 
         turned = psum.tile([P, S // P, P], F32, name="turned")
         chunks = planes[0][:, T:]

@@ -44,7 +44,7 @@ def tile_picked_modgate_linnone_l_kernel(tc, xT, gate, w1_words, w1_scales, offs
         w_scales = sb.tile([P, N], U8, name="w_scales", align_bytes=64)
         nc.gpsimd.memset(w_scales[:].bitcast(I32), 0)
         x_rows = xT.rearrange("(p j) t -> p j t", j=PACK)
-        tails = (S, 4, 0, HALF)
+        tails = (S, 4, 0, 0)
         planes = [sb.tile([P, T + tails[j]], F32, name=f"plane{j}") for j in range(PACK)]
         for j in range(PACK):
             nc.sync.dma_start(planes[j][:, 0:T], x_rows[:, j, :])
@@ -74,14 +74,10 @@ def tile_picked_modgate_linnone_l_kernel(tc, xT, gate, w1_words, w1_scales, offs
 
         woven = sb.tile([P, S * PACK], BF16, name="woven", align_bytes=64)
         values = woven[:].rearrange("p (s j) -> p s j", j=PACK)
-        score_halves = (planes[3][:, T:], planes[3][:, P : P + HALF])
+        scores = planes[3][:, 0:S]
 
-        def scores(lo, hi):
-            return score_halves[lo // HALF][:, lo % HALF : lo % HALF + hi - lo]
-
-        weighted = sb.tile([P, S], F32, name="weighted")
-        flat = weighted[:, 0:HALF].bitcast(BF16)
-        flat_pairs = flat.rearrange("p (h e s) -> p h s e", h=2, e=2)
+        weighted = sb.tile([P, N // P, S], F32, name="weighted")
+        flat = weighted[:].rearrange("p b s -> p (b s)").bitcast(BF16).rearrange("p (e s) -> p e s", e=2)
 
         def gather_a(j, lo, hi):
             nc.vector.tensor_copy(values[:, lo:hi, j], planes[j][:, 0 : (T + S if j == 0 else T)].indirect(entries(lo, hi)))
@@ -89,13 +85,12 @@ def tile_picked_modgate_linnone_l_kernel(tc, xT, gate, w1_words, w1_scales, offs
         def gather_b(j):
             cuts = CUTS[j // 2]
             for h in range(2):
-                base = h * HALF + (j % 2) * P
-                nc.scalar.activation(flat[:, base : base + cuts[h + 1] - cuts[h]], planes[j][:].indirect(entries(cuts[h], cuts[h + 1])), COPY)
+                nc.scalar.activation(flat[:, j % 2, h * HALF : h * HALF + cuts[h + 1] - cuts[h]], planes[j][:].indirect(entries(cuts[h], cuts[h + 1])), COPY)
 
         def weave(u, copy):
             cuts = CUTS[u]
             for h in range(2):
-                copy(values[:, cuts[h] : cuts[h + 1], 2 * u : 2 * u + 2], flat_pairs[:, h, 0 : cuts[h + 1] - cuts[h], :])
+                copy(values[:, cuts[h] : cuts[h + 1], 2 * u : 2 * u + 2], flat[:, :, h * HALF : h * HALF + cuts[h + 1] - cuts[h]].rearrange("p e s -> p s e"))
 
         x_codes = sb.tile([P, S], U32, name="x_codes", align_bytes=64)
         x_scales = sb.tile([P, S], U8, name="x_scales", align_bytes=64)
@@ -116,14 +111,11 @@ def tile_picked_modgate_linnone_l_kernel(tc, xT, gate, w1_words, w1_scales, offs
             )
             return acc[:]
 
-        plain = planes[3][:, 0:P]
-        weighted_rest = sb.tile([P, S - P], F32, name="weighted_rest")
-
-        def weigh(lo, hi):
-            nc.vector.tensor_tensor(weighted[:, lo:hi], multiply(0, lo, hi), scores(lo, hi), MULT)
+        def weigh(b, lo, hi, sums):
+            nc.vector.tensor_tensor(weighted[:, b, lo:hi], sums, scores[:, lo:hi], MULT)
 
         def scatter_first(lo, hi):
-            nc.scalar.activation(placed[0][:].indirect(entries(lo, hi)), weighted[:, lo:hi], COPY)
+            nc.scalar.activation(placed[0][:].indirect(entries(lo, hi)), weighted[:, 0, lo:hi], COPY)
 
         gather_a(0, 0, CUTS[0][0])
         gather_b(0)
@@ -134,7 +126,6 @@ def tile_picked_modgate_linnone_l_kernel(tc, xT, gate, w1_words, w1_scales, offs
         gather_a(1, 0, CUTS[0][0])
         gather_b(1)
         weave(0, nc.scalar.copy)
-        nc.scalar.copy(scores(0, HALF), spread[:, 0:HALF])
         gather_a(2, 0, CUTS[1][0])
         gather_b(2)
         gather_a(3, 0, P)
@@ -143,18 +134,20 @@ def tile_picked_modgate_linnone_l_kernel(tc, xT, gate, w1_words, w1_scales, offs
         for lo in (0, P):
             quantise(lo, lo + P)
         weave(1, nc.vector.tensor_copy)
-        nc.scalar.copy(scores(HALF, S), spread[:, HALF:S])
-        for lo in (0, P):
-            weigh(lo, lo + P)
-        quantise(HALF, S)
+        for lo, hi in ((0, P), (P, S)):
+            nc.scalar.copy(scores[:, lo:hi], spread[:, lo:hi])
+        first = [multiply(0, lo, lo + P) for lo in (0, P)]
         head = multiply(1, 0, HALF)
-        nc.scalar.copy(plain, head[:, 0:P])
-        scatter_first(0, HALF)
-        nc.vector.tensor_tensor(weighted_rest[:, 0:P], head[:, P:HALF], scores(P, HALF), MULT)
-        nc.vector.tensor_tensor(placed[1][:].indirect(entries(0, P)), plain, scores(0, P), MULT)
-        weigh(HALF, S)
-        nc.vector.tensor_tensor(weighted_rest[:, P:], multiply(1, HALF, S), scores(HALF, S), MULT)
-        scatter_first(HALF, S)
-        nc.vector.tensor_copy(placed[1][:].indirect(entries(P, S)), weighted_rest[:])
+        weigh(0, 0, P, first[0])
+        scatter_first(0, P)
+        for lo in (HALF, HALF + P):
+            quantise(lo, lo + P)
+        weigh(0, P, HALF, first[1])
+        weigh(1, 0, HALF, head)
+        for lo in (HALF, HALF + P):
+            weigh(0, lo, lo + P, multiply(0, lo, lo + P))
+        scatter_first(P, S)
+        weigh(1, HALF, S, multiply(1, HALF, S))
+        nc.vector.tensor_copy(placed[1][:].indirect(offsets[:]), weighted[:, 1, :])
         for b in range(N // P):
             nc.sync.dma_start(out[b * P : (b + 1) * P, :], placed[b][:])

@@ -146,8 +146,11 @@ def tile_picked_modgate_linnone_l_kernel(tc, xT, gate, w1_words, w1_scales, offs
         weigh(1, 0, HALF, head)
         for lo in (HALF, HALF + P):
             weigh(0, lo, lo + P, multiply(0, lo, lo + P))
+        last = multiply(1, HALF, S)
+        nc.scalar.copy(weighted[:, 1, HALF : HALF + P], last[:, 0:P])
         scatter_first(P, S)
-        weigh(1, HALF, S, multiply(1, HALF, S))
-        nc.vector.tensor_copy(placed[1][:].indirect(offsets[:]), weighted[:, 1, :])
+        nc.vector.tensor_copy(placed[1][:].indirect(entries(0, HALF)), weighted[:, 1, 0:HALF])
+        nc.vector.tensor_copy(weighted[:, 1, HALF + P : S], last[:, P:HALF])
+        nc.vector.tensor_tensor(placed[1][:].indirect(entries(HALF, S)), weighted[:, 1, HALF:S], scores[:, HALF:S], MULT)
         for b in range(N // P):
             nc.sync.dma_start(out[b * P : (b + 1) * P, :], placed[b][:])

@@ -21,7 +21,10 @@ P = 128
 PACK = 4
 HALF = 256
 STRIP = 64
-CUTS = ((320, 416, 512), (256, 384, 512))
+EARLY_CUT = 288
+LATE_CUTS = (128, 320)
+FIRST = S - P
+MIDDLE = FIRST + 64
 
 
 def tile_picked_modgate_linnone_l_kernel(tc, xT, gate, w1_words, w1_scales, offs, out):
@@ -33,8 +36,8 @@ def tile_picked_modgate_linnone_l_kernel(tc, xT, gate, w1_words, w1_scales, offs
         offsets = sb.tile([P, S // 16], U16, name="offsets")
         nc.sync.dma_start(offsets[:], offs)
         placed = [sb.tile([P, T], F32, name=f"placed{b}") for b in range(N // P)]
-        nc.vector.memset(placed[0][:], 0.0)
-        gate_row = sb.tile([P, T], F32, name="gate_row")
+        nc.vector.memset(placed[0][:, STRIP:T], 0.0)
+        gate_row = placed[1]
         nc.scalar.dma_start(gate_row[P - 1 : P, :], gate[0:1, :])
         nc.vector.memset(gate_row[0 : P - 1, :], 0.0)
 
@@ -44,11 +47,11 @@ def tile_picked_modgate_linnone_l_kernel(tc, xT, gate, w1_words, w1_scales, offs
         w_scales = sb.tile([P, N], U8, name="w_scales", align_bytes=64)
         nc.gpsimd.memset(w_scales[:].bitcast(I32), 0)
         x_rows = xT.rearrange("(p j) t -> p j t", j=PACK)
-        tails = (S, 4, 0, 0)
+        tails = (S, 4, 4, P)
         planes = [sb.tile([P, T + tails[j]], F32, name=f"plane{j}") for j in range(PACK)]
-        for j in range(PACK):
+        for j in (0, 2, 1, 3):
             nc.sync.dma_start(planes[j][:, 0:T], x_rows[:, j, :])
-            if j == 1:
+            if j == 2:
                 for q in range(4):
                     nc.sync.dma_start(w_scales[32 * q : 32 * q + 4, :].bitcast(I32), w1_scales[0, 4 * q : 4 * q + 4, :].bitcast(I32))
 
@@ -58,39 +61,32 @@ def tile_picked_modgate_linnone_l_kernel(tc, xT, gate, w1_words, w1_scales, offs
         identity = sb.tile([P, P], F32, name="identity")
         make_identity(nc, identity[:])
 
-        nc.scalar.copy(placed[1][:, 0:STRIP], placed[0][:, 0:STRIP])
-        nc.sync.dma_start(placed[1][:, STRIP:T], placed[0][:, STRIP:T])
+        nc.scalar.copy(placed[0][:, 0:STRIP], placed[0][:, STRIP : 2 * STRIP])
 
+        turned_first = psum.tile([P, P], F32, name="turned_first")
         turned = psum.tile([P, S // P, P], F32, name="turned")
         chunks = planes[0][:, T:]
-        for c in (0, 2, 1, 3):
+        for c in (3, 1, 2, 0):
             cols = slice(c * P, (c + 1) * P)
-            if c < 2:
+            if c >= 2:
                 nc.vector.tensor_copy(chunks[:, cols], gate_row[:].indirect(entries(c * P, (c + 1) * P)))
             else:
                 nc.scalar.activation(chunks[:, cols], gate_row[:].indirect(entries(c * P, (c + 1) * P)), COPY)
-            nc.tensor.transpose(turned[:, c, :], chunks[:, cols], identity[:])
-        score_cols = planes[1][:, T:]
+            nc.tensor.transpose(turned_first[:] if c == 3 else turned[:, c, :], chunks[:, cols], identity[:])
+        nc.sync.dma_start(placed[1][P - 1 : P, :], placed[1][0:1, :])
+        score_cols = planes[1][:, T : T + 3]
+        first_scores = planes[3][:, T:]
+        scores = sb.tile([P, FIRST], F32, name="scores")
 
         woven = sb.tile([P, S * PACK], BF16, name="woven", align_bytes=64)
         values = woven[:].rearrange("p (s j) -> p s j", j=PACK)
-        scores = planes[3][:, 0:S]
-
         weighted = sb.tile([P, N // P, S], F32, name="weighted")
-        flat = weighted[:].rearrange("p b s -> p (b s)").bitcast(BF16).rearrange("p (e s) -> p e s", e=2)
 
-        def gather_a(j, lo, hi):
-            nc.vector.tensor_copy(values[:, lo:hi, j], planes[j][:, 0 : (T + S if j == 0 else T)].indirect(entries(lo, hi)))
+        def gather_vector(j, lo, hi, width):
+            nc.vector.tensor_copy(values[:, lo:hi, j], planes[j][:, 0:width].indirect(entries(lo, hi)))
 
-        def gather_b(j):
-            cuts = CUTS[j // 2]
-            for h in range(2):
-                nc.scalar.activation(flat[:, j % 2, h * HALF : h * HALF + cuts[h + 1] - cuts[h]], planes[j][:].indirect(entries(cuts[h], cuts[h + 1])), COPY)
-
-        def weave(u, copy):
-            cuts = CUTS[u]
-            for h in range(2):
-                copy(values[:, cuts[h] : cuts[h + 1], 2 * u : 2 * u + 2], flat[:, :, h * HALF : h * HALF + cuts[h + 1] - cuts[h]].rearrange("p e s -> p s e"))
+        def gather_scalar(j, lo, hi):
+            nc.scalar.activation(values[:, lo:hi, j], planes[j][:].indirect(entries(lo, hi)), COPY)
 
         x_codes = sb.tile([P, S], U32, name="x_codes", align_bytes=64)
         x_scales = sb.tile([P, S], U8, name="x_scales", align_bytes=64)
@@ -98,10 +94,11 @@ def tile_picked_modgate_linnone_l_kernel(tc, xT, gate, w1_words, w1_scales, offs
         def quantise(lo, hi):
             nc.vector.quantize_mx(out=x_codes[:, lo:hi].bitcast(FP8X4), scales=x_scales[:, lo:hi], in_=woven[:, PACK * lo : PACK * hi])
 
-        def multiply(b, lo, hi):
-            acc = psum.tile([P, hi - lo], F32, name=f"acc{b}_{lo}")
+        def multiply(b, lo, hi, acc=None):
+            if acc is None:
+                acc = psum.tile([P, hi - lo], F32, name=f"acc{b}_{lo}")[:]
             nc.tensor.matmul_mx(
-                out=acc[:],
+                out=acc,
                 lhsT=w_codes[:, b * P : (b + 1) * P].bitcast(FP8X4),
                 lhsT_scale=w_scales[:, b * P : (b + 1) * P],
                 rhs=x_codes[:, lo:hi].bitcast(FP8X4),
@@ -109,48 +106,56 @@ def tile_picked_modgate_linnone_l_kernel(tc, xT, gate, w1_words, w1_scales, offs
                 start=True,
                 stop=True,
             )
-            return acc[:]
+            return acc
 
         def weigh(b, lo, hi, sums):
-            nc.vector.tensor_tensor(weighted[:, b, lo:hi], sums, scores[:, lo:hi], MULT)
+            nc.vector.tensor_tensor(weighted[:, b, lo:hi], sums, first_scores if lo == FIRST else scores[:, lo:hi], MULT)
 
         def scatter_first(lo, hi):
             nc.scalar.activation(placed[0][:].indirect(entries(lo, hi)), weighted[:, 0, lo:hi], COPY)
 
-        gather_a(0, 0, CUTS[0][0])
-        gather_b(0)
-        nc.scalar.copy(score_cols, turned[:, :, P - 1])
-        spread = psum.tile([P, S], F32, name="spread")
-        for i in range(S // P):
+        gather_vector(0, 0, EARLY_CUT, T + S)
+        gather_scalar(0, EARLY_CUT, S)
+        first_col = planes[2][:, T : T + 1]
+        nc.scalar.copy(first_col, turned_first[:, P - 1 : P])
+        nc.tensor.transpose(turned[:, 3, :], first_col.to_broadcast([P, P]), identity[:])
+        lo_cut, hi_cut = LATE_CUTS
+        gather_vector(2, lo_cut, hi_cut, T)
+        gather_scalar(2, hi_cut, S)
+        gather_scalar(2, 0, lo_cut)
+        nc.scalar.copy(score_cols, turned[:, 0:3, P - 1])
+        nc.scalar.copy(first_scores, turned[:, 3, :])
+        spread = psum.tile([P, FIRST], F32, name="spread")
+        for i in range(FIRST // P):
             nc.tensor.transpose(spread[:, i * P : (i + 1) * P], score_cols[:, i : i + 1].to_broadcast([P, P]), identity[:])
-        gather_a(1, 0, CUTS[0][0])
-        gather_b(1)
-        weave(0, nc.scalar.copy)
-        gather_a(2, 0, CUTS[1][0])
-        gather_b(2)
-        gather_a(3, 0, P)
-        gather_a(3, P, CUTS[1][0])
-        gather_b(3)
-        for lo in (0, P):
-            quantise(lo, lo + P)
-        weave(1, nc.vector.tensor_copy)
-        for lo, hi in ((0, P), (P, S)):
-            nc.scalar.copy(scores[:, lo:hi], spread[:, lo:hi])
-        first = [multiply(0, lo, lo + P) for lo in (0, P)]
-        head = multiply(1, 0, HALF)
-        weigh(0, 0, P, first[0])
-        scatter_first(0, P)
-        for lo in (HALF, HALF + P):
-            quantise(lo, lo + P)
-        weigh(0, P, HALF, first[1])
-        weigh(1, 0, HALF, head)
-        for lo in (HALF, HALF + P):
-            weigh(0, lo, lo + P, multiply(0, lo, lo + P))
-        last = multiply(1, HALF, S)
-        nc.scalar.copy(weighted[:, 1, HALF : HALF + P], last[:, 0:P])
-        scatter_first(P, S)
-        nc.vector.tensor_copy(placed[1][:].indirect(entries(0, HALF)), weighted[:, 1, 0:HALF])
-        nc.vector.tensor_copy(weighted[:, 1, HALF + P : S], last[:, P:HALF])
-        nc.vector.tensor_tensor(placed[1][:].indirect(entries(HALF, S)), weighted[:, 1, HALF:S], scores[:, HALF:S], MULT)
+        gather_vector(1, 0, EARLY_CUT, T)
+        gather_scalar(1, EARLY_CUT, S)
+        gather_vector(3, lo_cut, hi_cut, T)
+        gather_scalar(3, FIRST, MIDDLE)
+        gather_scalar(3, MIDDLE, S)
+        gather_scalar(3, hi_cut, FIRST)
+        gather_scalar(3, 0, lo_cut)
+        nc.scalar.copy(scores[:, 0:FIRST], spread[:])
+        quantise(FIRST, MIDDLE)
+        quantise(MIDDLE, S)
+        quantise(P, FIRST)
+        front = psum.tile([P, FIRST], F32, name="front")
+        multiply(0, FIRST, MIDDLE, front[:, 0:64])
+        multiply(0, MIDDLE, S, front[:, 64:P])
+        first = [front[:, 0:P], multiply(1, FIRST, S)]
+        second = [multiply(0, lo, lo + P) for lo in (HALF, P)]
+        quantise(0, P)
+        third = multiply(0, 0, P, turned_first[:])
+        weigh(0, FIRST, S, first[0])
+        nc.scalar.copy(weighted[:, 1, FIRST:S], first[1])
+        scatter_first(FIRST, S)
+        weigh(0, HALF, FIRST, second[0])
+        weigh(0, P, HALF, second[1])
+        weigh(0, 0, P, third)
+        nc.scalar.copy(weighted[:, 1, P:FIRST], multiply(1, P, FIRST, front[:, P:FIRST]))
+        scatter_first(0, FIRST)
+        nc.vector.tensor_tensor(placed[1][:].indirect(entries(FIRST, S)), weighted[:, 1, FIRST:S], first_scores, MULT)
+        nc.vector.tensor_copy(weighted[:, 1, 0:P], multiply(1, 0, P, turned[:, 0, :]))
+        nc.vector.tensor_tensor(placed[1][:].indirect(entries(0, FIRST)), weighted[:, 1, 0:FIRST], scores[:, 0:FIRST], MULT)
         for b in range(N // P):
-            nc.sync.dma_start(out[b * P : (b + 1) * P, :], placed[b][:])
+            (nc.scalar, nc.sync)[b].dma_start(out[b * P : (b + 1) * P, :], placed[b][:])

@@ -109,7 +109,7 @@ def tile_picked_modgate_linnone_l_kernel(tc, xT, gate, w1_words, w1_scales, offs
             return acc
 
         def weigh(b, lo, hi, sums):
-            nc.vector.tensor_tensor(weighted[:, b, lo:hi], sums, first_scores if lo == FIRST else scores[:, lo:hi], MULT)
+            nc.vector.tensor_tensor(weighted[:, b, lo:hi], sums, first_scores[:, lo - FIRST : hi - FIRST] if lo >= FIRST else scores[:, lo:hi], MULT)
 
         def scatter_first(lo, hi):
             nc.scalar.activation(placed[0][:].indirect(entries(lo, hi)), weighted[:, 0, lo:hi], COPY)
@@ -134,19 +134,21 @@ def tile_picked_modgate_linnone_l_kernel(tc, xT, gate, w1_words, w1_scales, offs
         gather_scalar(3, FIRST, MIDDLE)
         gather_scalar(3, MIDDLE, S)
         gather_scalar(3, hi_cut, FIRST)
-        gather_scalar(3, 0, lo_cut)
+        gather_scalar(3, 64, lo_cut)
+        gather_scalar(3, 0, 64)
         nc.scalar.copy(scores[:, 0:FIRST], spread[:])
         quantise(FIRST, MIDDLE)
         quantise(MIDDLE, S)
         quantise(P, FIRST)
         front = psum.tile([P, FIRST], F32, name="front")
-        multiply(0, FIRST, MIDDLE, front[:, 0:64])
-        multiply(0, MIDDLE, S, front[:, 64:P])
-        first = [front[:, 0:P], multiply(1, FIRST, S)]
+        early = multiply(0, FIRST, MIDDLE)
+        first = [multiply(0, MIDDLE, S, front[:, 0:64]), multiply(1, FIRST, S)]
         second = [multiply(0, lo, lo + P) for lo in (HALF, P)]
-        quantise(0, P)
+        quantise(64, P)
+        weigh(0, FIRST, MIDDLE, early)
+        quantise(0, 64)
         third = multiply(0, 0, P, turned_first[:])
-        weigh(0, FIRST, S, first[0])
+        weigh(0, MIDDLE, S, first[0])
         nc.scalar.copy(weighted[:, 1, FIRST:S], first[1])
         scatter_first(FIRST, S)
         weigh(0, HALF, FIRST, second[0])

@@ -19,10 +19,10 @@ COPY = mybir.ActivationFunctionType.Copy
 
 P = 128
 PACK = 4
-HALF = 256
+ROW_ALIGN = 256
 STRIP = 64
 EARLY_CUT = 288
-LATE_CUTS = (128, 320)
+LATE_LO, LATE_HI = 128, 320
 FIRST = S - P
 MIDDLE = FIRST + 64
 
@@ -35,32 +35,32 @@ def tile_picked_modgate_linnone_l_kernel(tc, xT, gate, w1_words, w1_scales, offs
 
         offsets = sb.tile([P, S // 16], U16, name="offsets")
         nc.sync.dma_start(offsets[:], offs)
-        placed = [sb.tile([P, T], F32, name=f"placed{b}") for b in range(N // P)]
+
+        def entries(lo, hi):
+            return offsets[:, lo // 16 : hi // 16]
+
+        placed = [sb.tile([P, T], F32, name=f"placed{b}", align_bytes=ROW_ALIGN) for b in range(N // P)]
         nc.vector.memset(placed[0][:, STRIP:T], 0.0)
         gate_row = placed[1]
         nc.scalar.dma_start(gate_row[P - 1 : P, :], gate[0:1, :])
         nc.vector.memset(gate_row[0 : P - 1, :], 0.0)
 
-        def entries(lo, hi):
-            return offsets[:, lo // 16 : hi // 16]
-
         w_scales = sb.tile([P, N], U8, name="w_scales", align_bytes=64)
         nc.gpsimd.memset(w_scales[:].bitcast(I32), 0)
+
         x_rows = xT.rearrange("(p j) t -> p j t", j=PACK)
         tails = (S, 4, 4, P)
-        planes = [sb.tile([P, T + tails[j]], F32, name=f"plane{j}") for j in range(PACK)]
+        planes = [sb.tile([P, T + tails[j]], F32, name=f"plane{j}", align_bytes=ROW_ALIGN) for j in range(PACK)]
         for j in (0, 2, 1, 3):
             nc.sync.dma_start(planes[j][:, 0:T], x_rows[:, j, :])
             if j == 2:
                 for q in range(4):
                     nc.sync.dma_start(w_scales[32 * q : 32 * q + 4, :].bitcast(I32), w1_scales[0, 4 * q : 4 * q + 4, :].bitcast(I32))
-
-        w_codes = sb.tile([P, N], U32, name="w_codes", align_bytes=64)
+        w_codes = sb.tile([P, N], U32, name="w_codes", align_bytes=ROW_ALIGN)
         nc.sync.dma_start(w_codes[:].bitcast(I32), w1_words[0].rearrange("p n t -> p (n t)").bitcast(I32))
 
         identity = sb.tile([P, P], F32, name="identity")
         make_identity(nc, identity[:])
-
         nc.scalar.copy(placed[0][:, 0:STRIP], placed[0][:, STRIP : 2 * STRIP])
 
         turned_first = psum.tile([P, P], F32, name="turned_first")
@@ -74,13 +74,15 @@ def tile_picked_modgate_linnone_l_kernel(tc, xT, gate, w1_words, w1_scales, offs
                 nc.scalar.activation(chunks[:, cols], gate_row[:].indirect(entries(c * P, (c + 1) * P)), COPY)
             nc.tensor.transpose(turned_first[:] if c == 3 else turned[:, c, :], chunks[:, cols], identity[:])
         nc.sync.dma_start(placed[1][P - 1 : P, :], placed[1][0:1, :])
+
         score_cols = planes[1][:, T : T + 3]
         first_scores = planes[3][:, T:]
         scores = sb.tile([P, FIRST], F32, name="scores")
-
         woven = sb.tile([P, S * PACK], BF16, name="woven", align_bytes=64)
         values = woven[:].rearrange("p (s j) -> p s j", j=PACK)
         weighted = sb.tile([P, N // P, S], F32, name="weighted")
+        x_codes = sb.tile([P, S], U32, name="x_codes", align_bytes=64)
+        x_scales = sb.tile([P, S], U8, name="x_scales", align_bytes=64)
 
         def gather_vector(j, lo, hi, width):
             nc.vector.tensor_copy(values[:, lo:hi, j], planes[j][:, 0:width].indirect(entries(lo, hi)))
@@ -88,15 +90,10 @@ def tile_picked_modgate_linnone_l_kernel(tc, xT, gate, w1_words, w1_scales, offs
         def gather_scalar(j, lo, hi):
             nc.scalar.activation(values[:, lo:hi, j], planes[j][:].indirect(entries(lo, hi)), COPY)
 
-        x_codes = sb.tile([P, S], U32, name="x_codes", align_bytes=64)
-        x_scales = sb.tile([P, S], U8, name="x_scales", align_bytes=64)
-
         def quantise(lo, hi):
             nc.vector.quantize_mx(out=x_codes[:, lo:hi].bitcast(FP8X4), scales=x_scales[:, lo:hi], in_=woven[:, PACK * lo : PACK * hi])
 
-        def multiply(b, lo, hi, acc=None):
-            if acc is None:
-                acc = psum.tile([P, hi - lo], F32, name=f"acc{b}_{lo}")[:]
+        def multiply(b, lo, hi, acc):
             nc.tensor.matmul_mx(
                 out=acc,
                 lhsT=w_codes[:, b * P : (b + 1) * P].bitcast(FP8X4),
@@ -108,21 +105,20 @@ def tile_picked_modgate_linnone_l_kernel(tc, xT, gate, w1_words, w1_scales, offs
             )
             return acc
 
-        def weigh(b, lo, hi, sums):
-            nc.vector.tensor_tensor(weighted[:, b, lo:hi], sums, first_scores[:, lo - FIRST : hi - FIRST] if lo >= FIRST else scores[:, lo:hi], MULT)
+        def bank(name, width):
+            return psum.tile([P, width], F32, name=name)[:]
 
-        def scatter_first(lo, hi):
-            nc.scalar.activation(placed[0][:].indirect(entries(lo, hi)), weighted[:, 0, lo:hi], COPY)
+        def weigh(lo, hi, sums):
+            nc.vector.tensor_tensor(weighted[:, 0, lo:hi], sums, first_scores[:, lo - FIRST : hi - FIRST] if lo >= FIRST else scores[:, lo:hi], MULT)
 
         gather_vector(0, 0, EARLY_CUT, T + S)
         gather_scalar(0, EARLY_CUT, S)
         first_col = planes[2][:, T : T + 1]
         nc.scalar.copy(first_col, turned_first[:, P - 1 : P])
         nc.tensor.transpose(turned[:, 3, :], first_col.to_broadcast([P, P]), identity[:])
-        lo_cut, hi_cut = LATE_CUTS
-        gather_vector(2, lo_cut, hi_cut, T)
-        gather_scalar(2, hi_cut, S)
-        gather_scalar(2, 0, lo_cut)
+        gather_vector(2, LATE_LO, LATE_HI, T)
+        gather_scalar(2, LATE_HI, S)
+        gather_scalar(2, 0, LATE_LO)
         nc.scalar.copy(score_cols, turned[:, 0:3, P - 1])
         nc.scalar.copy(first_scores, turned[:, 3, :])
         spread = psum.tile([P, FIRST], F32, name="spread")
@@ -130,34 +126,32 @@ def tile_picked_modgate_linnone_l_kernel(tc, xT, gate, w1_words, w1_scales, offs
             nc.tensor.transpose(spread[:, i * P : (i + 1) * P], score_cols[:, i : i + 1].to_broadcast([P, P]), identity[:])
         gather_vector(1, 0, EARLY_CUT, T)
         gather_scalar(1, EARLY_CUT, S)
-        gather_vector(3, lo_cut, hi_cut, T)
-        gather_scalar(3, FIRST, MIDDLE)
-        gather_scalar(3, MIDDLE, S)
-        gather_scalar(3, hi_cut, FIRST)
-        gather_scalar(3, 64, lo_cut)
-        gather_scalar(3, 0, 64)
-        nc.scalar.copy(scores[:, 0:FIRST], spread[:])
-        quantise(FIRST, MIDDLE)
-        quantise(MIDDLE, S)
-        quantise(P, FIRST)
-        front = psum.tile([P, FIRST], F32, name="front")
-        early = multiply(0, FIRST, MIDDLE)
-        first = [multiply(0, MIDDLE, S, front[:, 0:64]), multiply(1, FIRST, S)]
-        second = [multiply(0, lo, lo + P) for lo in (HALF, P)]
-        quantise(64, P)
-        weigh(0, FIRST, MIDDLE, early)
-        quantise(0, 64)
-        third = multiply(0, 0, P, turned_first[:])
-        weigh(0, MIDDLE, S, first[0])
-        nc.scalar.copy(weighted[:, 1, FIRST:S], first[1])
-        scatter_first(FIRST, S)
-        weigh(0, HALF, FIRST, second[0])
-        weigh(0, P, HALF, second[1])
-        weigh(0, 0, P, third)
-        nc.scalar.copy(weighted[:, 1, P:FIRST], multiply(1, P, FIRST, front[:, P:FIRST]))
-        scatter_first(0, FIRST)
+
+        gather_vector(3, LATE_LO, LATE_HI, T)
+        for lo in (FIRST, MIDDLE, LATE_HI, 64, 0):
+            gather_scalar(3, lo, lo + 64)
+        nc.scalar.copy(scores[:], spread[:])
+        for lo, hi in ((FIRST, MIDDLE), (MIDDLE, S), (P, FIRST), (64, P), (0, 64)):
+            quantise(lo, hi)
+
+        shared = bank("shared", 2 * P)
+        sums_a = multiply(0, FIRST, MIDDLE, bank("sums_a", 64))
+        sums_b = multiply(0, MIDDLE, S, shared[:, 0:64])
+        other_first = multiply(1, FIRST, S, bank("other_first", P))
+        middle = [multiply(0, lo, lo + P, bank(f"middle{lo}", P)) for lo in (2 * P, P)]
+        last = multiply(0, 0, P, turned_first[:])
+        weigh(FIRST, MIDDLE, sums_a)
+        weigh(MIDDLE, S, sums_b)
+        nc.scalar.copy(weighted[:, 1, FIRST:S], other_first)
+        nc.scalar.activation(placed[0][:].indirect(entries(FIRST, S)), weighted[:, 0, FIRST:S], COPY)
+        weigh(2 * P, FIRST, middle[0])
+        weigh(P, 2 * P, middle[1])
+        weigh(0, P, last)
+        nc.scalar.copy(weighted[:, 1, 2 * P : FIRST], multiply(1, 2 * P, FIRST, shared[:, P : 2 * P]))
+        nc.scalar.activation(placed[0][:].indirect(entries(0, FIRST)), weighted[:, 0, 0:FIRST], COPY)
         nc.vector.tensor_tensor(placed[1][:].indirect(entries(FIRST, S)), weighted[:, 1, FIRST:S], first_scores, MULT)
-        nc.vector.tensor_copy(weighted[:, 1, 0:P], multiply(1, 0, P, turned[:, 0, :]))
-        nc.vector.tensor_tensor(placed[1][:].indirect(entries(0, FIRST)), weighted[:, 1, 0:FIRST], scores[:, 0:FIRST], MULT)
+        other_rest = turned[:, 0:2, :].rearrange("p c n -> p (c n)")
+        nc.vector.tensor_copy(weighted[:, 1, 0 : 2 * P], multiply(1, 0, 2 * P, other_rest))
+        nc.vector.tensor_tensor(placed[1][:].indirect(entries(0, FIRST)), weighted[:, 1, 0:FIRST], scores[:], MULT)
         for b in range(N // P):
             (nc.scalar, nc.sync)[b].dma_start(out[b * P : (b + 1) * P, :], placed[b][:])

@@ -21,8 +21,10 @@ P = 128
 PACK = 4
 ROW_ALIGN = 256
 STRIP = 64
-EARLY_CUT = 288
-LATE_LO, LATE_HI = 128, 320
+RUN = 64
+PAIRED = 3
+OWN = PAIRED * RUN
+EARLY_CUT = OWN + 2 * RUN
 FIRST = S - P
 MIDDLE = FIRST + 64
 
@@ -84,11 +86,19 @@ def tile_picked_modgate_linnone_l_kernel(tc, xT, gate, w1_words, w1_scales, offs
         x_codes = sb.tile([P, S], U32, name="x_codes", align_bytes=64)
         x_scales = sb.tile([P, S], U8, name="x_scales", align_bytes=64)
 
-        def gather_vector(j, lo, hi, width):
-            nc.vector.tensor_copy(values[:, lo:hi, j], planes[j][:, 0:width].indirect(entries(lo, hi)))
+        paired = woven[:, 0 : FIRST * PACK].rearrange("p (i h n j) -> p h i n j", i=PAIRED, h=2, j=PACK)
 
-        def gather_scalar(j, lo, hi):
-            nc.scalar.activation(values[:, lo:hi, j], planes[j][:].indirect(entries(lo, hi)), COPY)
+        def gather_vector(j, target, lo, hi, width):
+            nc.vector.tensor_copy(target, planes[j][:, 0:width].indirect(entries(lo, hi)))
+
+        def gather_scalar(j, target, lo, hi):
+            nc.scalar.activation(target, planes[j][:].indirect(entries(lo, hi)), COPY)
+
+        def by_piece(row):
+            return row.rearrange("p (h i n) -> p i h n", h=2, i=PAIRED)
+
+        def halves(sums):
+            return sums.rearrange("p (h n) -> p h n", h=2)
 
         def quantise(lo, hi):
             nc.vector.quantize_mx(out=x_codes[:, lo:hi].bitcast(FP8X4), scales=x_scales[:, lo:hi], in_=woven[:, PACK * lo : PACK * hi])
@@ -108,50 +118,64 @@ def tile_picked_modgate_linnone_l_kernel(tc, xT, gate, w1_words, w1_scales, offs
         def bank(name, width):
             return psum.tile([P, width], F32, name=name)[:]
 
-        def weigh(lo, hi, sums):
-            nc.vector.tensor_tensor(weighted[:, 0, lo:hi], sums, first_scores[:, lo - FIRST : hi - FIRST] if lo >= FIRST else scores[:, lo:hi], MULT)
+        def weigh_first(lo, hi, sums):
+            nc.vector.tensor_tensor(weighted[:, 0, lo:hi], sums, first_scores[:, lo - FIRST : hi - FIRST], MULT)
 
-        gather_vector(0, 0, EARLY_CUT, T + S)
-        gather_scalar(0, EARLY_CUT, S)
+        def weigh(i, sums):
+            nc.vector.tensor_tensor(by_piece(weighted[:, 0, 0:FIRST])[:, i], halves(sums), by_piece(scores[:])[:, i], MULT)
+
+        def early_plane(j, width):
+            gather_vector(j, paired[:, 0, :, :, j], 0, OWN, width)
+            gather_vector(j, paired[:, 1, 0:2, :, j], OWN, EARLY_CUT, T)
+            gather_scalar(j, values[:, EARLY_CUT:S, j], EARLY_CUT, S)
+
+        early_plane(0, T + S)
         first_col = planes[2][:, T : T + 1]
         nc.scalar.copy(first_col, turned_first[:, P - 1 : P])
         nc.tensor.transpose(turned[:, 3, :], first_col.to_broadcast([P, P]), identity[:])
-        gather_vector(2, LATE_LO, LATE_HI, T)
-        gather_scalar(2, LATE_HI, S)
-        gather_scalar(2, 0, LATE_LO)
+        gather_vector(2, paired[:, 0, :, :, 2], 0, OWN, T)
+        gather_scalar(2, values[:, EARLY_CUT:S, 2], EARLY_CUT, S)
+        for i in range(2):
+            gather_scalar(2, paired[:, 1, i, :, 2], OWN + i * RUN, OWN + (i + 1) * RUN)
         nc.scalar.copy(score_cols, turned[:, 0:3, P - 1])
         nc.scalar.copy(first_scores, turned[:, 3, :])
         spread = psum.tile([P, FIRST], F32, name="spread")
         for i in range(FIRST // P):
             nc.tensor.transpose(spread[:, i * P : (i + 1) * P], score_cols[:, i : i + 1].to_broadcast([P, P]), identity[:])
-        gather_vector(1, 0, EARLY_CUT, T)
-        gather_scalar(1, EARLY_CUT, S)
+        early_plane(1, T)
 
-        gather_vector(3, LATE_LO, LATE_HI, T)
-        for lo in (FIRST, MIDDLE, LATE_HI, 64, 0):
-            gather_scalar(3, lo, lo + 64)
+        gather_vector(3, paired[:, 0, :, :, 3], 0, OWN, T)
+        gather_scalar(3, values[:, FIRST:MIDDLE, 3], FIRST, MIDDLE)
+        gather_scalar(3, values[:, MIDDLE:S, 3], MIDDLE, S)
+        for i in (2, 0, 1):
+            gather_scalar(3, paired[:, 1, i, :, 3], OWN + i * RUN, OWN + (i + 1) * RUN)
         nc.scalar.copy(scores[:], spread[:])
-        for lo, hi in ((FIRST, MIDDLE), (MIDDLE, S), (P, FIRST), (64, P), (0, 64)):
-            quantise(lo, hi)
+        quantise(FIRST, MIDDLE)
+        quantise(MIDDLE, S)
+        for i in (2, 0, 1):
+            quantise(i * P, (i + 1) * P)
 
         shared = bank("shared", 2 * P)
         sums_a = multiply(0, FIRST, MIDDLE, bank("sums_a", 64))
         sums_b = multiply(0, MIDDLE, S, shared[:, 0:64])
         other_first = multiply(1, FIRST, S, bank("other_first", P))
-        middle = [multiply(0, lo, lo + P, bank(f"middle{lo}", P)) for lo in (2 * P, P)]
-        last = multiply(0, 0, P, turned_first[:])
-        weigh(FIRST, MIDDLE, sums_a)
-        weigh(MIDDLE, S, sums_b)
+        second = multiply(0, 2 * P, FIRST, bank("second", P))
+        other_second = multiply(1, 2 * P, FIRST, turned[:, 0, :])
+        third_bank = bank("third_bank", 2 * P)
+        third = multiply(0, 0, P, third_bank[:, 0:P])
+        last = multiply(0, P, 2 * P, turned_first[:])
+        weigh_first(FIRST, MIDDLE, sums_a)
+        weigh_first(MIDDLE, S, sums_b)
         nc.scalar.copy(weighted[:, 1, FIRST:S], other_first)
         nc.scalar.activation(placed[0][:].indirect(entries(FIRST, S)), weighted[:, 0, FIRST:S], COPY)
-        weigh(2 * P, FIRST, middle[0])
-        weigh(P, 2 * P, middle[1])
-        weigh(0, P, last)
-        nc.scalar.copy(weighted[:, 1, 2 * P : FIRST], multiply(1, 2 * P, FIRST, shared[:, P : 2 * P]))
+        weigh(2, second)
+        nc.vector.tensor_copy(by_piece(weighted[:, 1, 0:FIRST])[:, 2], halves(other_second))
+        weigh(0, third)
+        weigh(1, last)
+        nc.scalar.copy(by_piece(weighted[:, 1, 0:FIRST])[:, 0], halves(multiply(1, 0, P, shared[:, P : 2 * P])))
         nc.scalar.activation(placed[0][:].indirect(entries(0, FIRST)), weighted[:, 0, 0:FIRST], COPY)
         nc.vector.tensor_tensor(placed[1][:].indirect(entries(FIRST, S)), weighted[:, 1, FIRST:S], first_scores, MULT)
-        other_rest = turned[:, 0:2, :].rearrange("p c n -> p (c n)")
-        nc.vector.tensor_copy(weighted[:, 1, 0 : 2 * P], multiply(1, 0, 2 * P, other_rest))
+        nc.vector.tensor_copy(by_piece(weighted[:, 1, 0:FIRST])[:, 1], halves(multiply(1, P, 2 * P, third_bank[:, P : 2 * P])))
         nc.vector.tensor_tensor(placed[1][:].indirect(entries(0, FIRST)), weighted[:, 1, 0:FIRST], scores[:], MULT)
         for b in range(N // P):
             (nc.scalar, nc.sync)[b].dma_start(out[b * P : (b + 1) * P, :], placed[b][:])

@@ -152,7 +152,7 @@ def tile_picked_modgate_linnone_l_kernel(tc, xT, gate, w1_words, w1_scales, offs
         nc.scalar.copy(scores[:], spread[:])
         quantise(FIRST, MIDDLE)
         quantise(MIDDLE, S)
-        for i in (2, 0, 1):
+        for i in (2, 0):
             quantise(i * P, (i + 1) * P)
 
         shared = bank("shared", 2 * P)
@@ -163,8 +163,9 @@ def tile_picked_modgate_linnone_l_kernel(tc, xT, gate, w1_words, w1_scales, offs
         other_second = multiply(1, 2 * P, FIRST, turned[:, 0, :])
         third_bank = bank("third_bank", 2 * P)
         third = multiply(0, 0, P, third_bank[:, 0:P])
-        last = multiply(0, P, 2 * P, turned_first[:])
         weigh_first(FIRST, MIDDLE, sums_a)
+        quantise(P, 2 * P)
+        last = multiply(0, P, 2 * P, turned_first[:])
         weigh_first(MIDDLE, S, sums_b)
         nc.scalar.copy(weighted[:, 1, FIRST:S], other_first)
         nc.scalar.activation(placed[0][:].indirect(entries(FIRST, S)), weighted[:, 0, FIRST:S], COPY)

from contextlib import ExitStack

import concourse.mybir as mybir
from concourse.masks import make_identity

K, T, S, N = 512, 1024, 512, 256
FLOPS = 2 * K * S * N
BYTES = 4 * K * T + 4 * T + K * N + K * N // 32 + 2 * 128 * S // 16 + 4 * N * T

F32 = mybir.dt.float32
BF16 = mybir.dt.bfloat16
I32 = mybir.dt.int32
U32 = mybir.dt.uint32
U16 = mybir.dt.uint16
U8 = mybir.dt.uint8
FP8X4 = mybir.dt.float8_e4m3fn_x4
MULT = mybir.AluOpType.mult
COPY = mybir.ActivationFunctionType.Copy

P = 128
PACK = 4
ROW_ALIGN = 256
STRIP = 64
RUN = 64
PAIRED = 3
OWN = PAIRED * RUN
EARLY_CUT = OWN + 2 * RUN
FIRST = S - P
MIDDLE = FIRST + 64


def tile_picked_modgate_linnone_l_kernel(tc, xT, gate, w1_words, w1_scales, offs, out):
    nc = tc.nc
    with ExitStack() as ctx:
        sb = ctx.enter_context(tc.tile_pool(name="sb", bufs=1))
        psum = ctx.enter_context(tc.psum_pool(name="psum", bufs=1))

        offsets = sb.tile([P, S // 16], U16, name="offsets")
        nc.sync.dma_start(offsets[:], offs)

        def entries(lo, hi):
            return offsets[:, lo // 16 : hi // 16]

        placed = [sb.tile([P, T], F32, name=f"placed{b}", align_bytes=ROW_ALIGN) for b in range(N // P)]
        nc.vector.memset(placed[0][:, STRIP:T], 0.0)
        gate_row = placed[1]
        nc.scalar.dma_start(gate_row[P - 1 : P, :], gate[0:1, :])
        nc.vector.memset(gate_row[0 : P - 1, :], 0.0)

        w_scales = sb.tile([P, N], U8, name="w_scales", align_bytes=64)
        nc.gpsimd.memset(w_scales[:].bitcast(I32), 0)

        x_rows = xT.rearrange("(p j) t -> p j t", j=PACK)
        tails = (S, 4, 4, P)
        planes = [sb.tile([P, T + tails[j]], F32, name=f"plane{j}", align_bytes=ROW_ALIGN) for j in range(PACK)]
        for j in (0, 2, 1, 3):
            nc.sync.dma_start(planes[j][:, 0:T], x_rows[:, j, :])
            if j == 2:
                for q in range(4):
                    nc.sync.dma_start(w_scales[32 * q : 32 * q + 4, :].bitcast(I32), w1_scales[0, 4 * q : 4 * q + 4, :].bitcast(I32))
        w_codes = sb.tile([P, N], U32, name="w_codes", align_bytes=ROW_ALIGN)
        nc.sync.dma_start(w_codes[:].bitcast(I32), w1_words[0].rearrange("p n t -> p (n t)").bitcast(I32))

        identity = sb.tile([P, P], F32, name="identity")
        make_identity(nc, identity[:])
        nc.scalar.copy(placed[0][:, 0:STRIP], placed[0][:, STRIP : 2 * STRIP])

        turned_first = psum.tile([P, P], F32, name="turned_first")
        turned = psum.tile([P, S // P, P], F32, name="turned")
        chunks = planes[0][:, T:]
        for c in (3, 1, 2, 0):
            cols = slice(c * P, (c + 1) * P)
            if c >= 2:
                nc.vector.tensor_copy(chunks[:, cols], gate_row[:].indirect(entries(c * P, (c + 1) * P)))
            else:
                nc.scalar.activation(chunks[:, cols], gate_row[:].indirect(entries(c * P, (c + 1) * P)), COPY)
            nc.tensor.transpose(turned_first[:] if c == 3 else turned[:, c, :], chunks[:, cols], identity[:])
        nc.sync.dma_start(placed[1][P - 1 : P, :], placed[1][0:1, :])

        score_cols = planes[1][:, T : T + 3]
        first_scores = planes[3][:, T:]
        scores = sb.tile([P, FIRST], F32, name="scores")
        woven = sb.tile([P, S * PACK], BF16, name="woven", align_bytes=64)
        values = woven[:].rearrange("p (s j) -> p s j", j=PACK)
        weighted = sb.tile([P, N // P, S], F32, name="weighted")
        x_codes = sb.tile([P, S], U32, name="x_codes", align_bytes=64)
        x_scales = sb.tile([P, S], U8, name="x_scales", align_bytes=64)

        paired = woven[:, 0 : FIRST * PACK].rearrange("p (i h n j) -> p h i n j", i=PAIRED, h=2, j=PACK)

        def gather_vector(j, target, lo, hi, width):
            nc.vector.tensor_copy(target, planes[j][:, 0:width].indirect(entries(lo, hi)))

        def gather_scalar(j, target, lo, hi):
            nc.scalar.activation(target, planes[j][:].indirect(entries(lo, hi)), COPY)

        def by_piece(row):
            return row.rearrange("p (h i n) -> p i h n", h=2, i=PAIRED)

        def halves(sums):
            return sums.rearrange("p (h n) -> p h n", h=2)

        def quantise(lo, hi):
            nc.vector.quantize_mx(out=x_codes[:, lo:hi].bitcast(FP8X4), scales=x_scales[:, lo:hi], in_=woven[:, PACK * lo : PACK * hi])

        def multiply(b, lo, hi, acc):
            nc.tensor.matmul_mx(
                out=acc,
                lhsT=w_codes[:, b * P : (b + 1) * P].bitcast(FP8X4),
                lhsT_scale=w_scales[:, b * P : (b + 1) * P],
                rhs=x_codes[:, lo:hi].bitcast(FP8X4),
                rhs_scale=x_scales[:, lo:hi],
                start=True,
                stop=True,
            )
            return acc

        def bank(name, width):
            return psum.tile([P, width], F32, name=name)[:]

        def weigh_first(lo, hi, sums):
            nc.vector.tensor_tensor(weighted[:, 0, lo:hi], sums, first_scores[:, lo - FIRST : hi - FIRST], MULT)

        def weigh(i, sums):
            nc.vector.tensor_tensor(by_piece(weighted[:, 0, 0:FIRST])[:, i], halves(sums), by_piece(scores[:])[:, i], MULT)

        def early_plane(j, width):
            gather_vector(j, paired[:, 0, :, :, j], 0, OWN, width)
            gather_vector(j, paired[:, 1, 0:2, :, j], OWN, EARLY_CUT, T)
            gather_scalar(j, values[:, EARLY_CUT:S, j], EARLY_CUT, S)

        early_plane(0, T + S)
        first_col = planes[2][:, T : T + 1]
        nc.scalar.copy(first_col, turned_first[:, P - 1 : P])
        nc.tensor.transpose(turned[:, 3, :], first_col.to_broadcast([P, P]), identity[:])
        gather_vector(2, paired[:, 0, :, :, 2], 0, OWN, T)
        gather_scalar(2, values[:, EARLY_CUT:S, 2], EARLY_CUT, S)
        for i in range(2):
            gather_scalar(2, paired[:, 1, i, :, 2], OWN + i * RUN, OWN + (i + 1) * RUN)
        nc.scalar.copy(score_cols, turned[:, 0:3, P - 1])
        nc.scalar.copy(first_scores, turned[:, 3, :])
        spread = psum.tile([P, FIRST], F32, name="spread")
        for i in range(FIRST // P):
            nc.tensor.transpose(spread[:, i * P : (i + 1) * P], score_cols[:, i : i + 1].to_broadcast([P, P]), identity[:])
        early_plane(1, T)

        gather_vector(3, paired[:, 0, :, :, 3], 0, OWN, T)
        gather_scalar(3, values[:, FIRST:MIDDLE, 3], FIRST, MIDDLE)
        gather_scalar(3, values[:, MIDDLE:S, 3], MIDDLE, S)
        for i in (2, 0, 1):
            gather_scalar(3, paired[:, 1, i, :, 3], OWN + i * RUN, OWN + (i + 1) * RUN)
        nc.scalar.copy(scores[:], spread[:])
        quantise(FIRST, MIDDLE)
        quantise(MIDDLE, S)
        for i in (2, 0):
            quantise(i * P, (i + 1) * P)

        shared = bank("shared", 2 * P)
        sums_a = multiply(0, FIRST, MIDDLE, bank("sums_a", 64))
        sums_b = multiply(0, MIDDLE, S, shared[:, 0:64])
        other_first = multiply(1, FIRST, S, bank("other_first", P))
        second = multiply(0, 2 * P, FIRST, bank("second", P))
        other_second = multiply(1, 2 * P, FIRST, turned[:, 0, :])
        third_bank = bank("third_bank", 2 * P)
        third = multiply(0, 0, P, third_bank[:, 0:P])
        weigh_first(FIRST, MIDDLE, sums_a)
        quantise(P, 2 * P)
        last = multiply(0, P, 2 * P, turned_first[:])
        weigh_first(MIDDLE, S, sums_b)
        nc.scalar.copy(weighted[:, 1, FIRST:S], other_first)
        nc.scalar.activation(placed[0][:].indirect(entries(FIRST, S)), weighted[:, 0, FIRST:S], COPY)
        weigh(2, second)
        nc.vector.tensor_copy(by_piece(weighted[:, 1, 0:FIRST])[:, 2], halves(other_second))
        weigh(0, third)
        weigh(1, last)
        nc.scalar.copy(by_piece(weighted[:, 1, 0:FIRST])[:, 0], halves(multiply(1, 0, P, shared[:, P : 2 * P])))
        nc.scalar.activation(placed[0][:].indirect(entries(0, FIRST)), weighted[:, 0, 0:FIRST], COPY)
        nc.vector.tensor_tensor(placed[1][:].indirect(entries(FIRST, S)), weighted[:, 1, FIRST:S], first_scores, MULT)
        nc.vector.tensor_copy(by_piece(weighted[:, 1, 0:FIRST])[:, 1], halves(multiply(1, P, 2 * P, third_bank[:, P : 2 * P])))
        nc.vector.tensor_tensor(placed[1][:].indirect(entries(0, FIRST)), weighted[:, 1, 0:FIRST], scores[:], MULT)
        for b in range(N // P):
            (nc.scalar, nc.sync)[b].dma_start(out[b * P : (b + 1) * P, :], placed[b][:])
